import numpy as np, ml_dtypes
CORES = [16,18,20,22]
N = 4
BF = ml_dtypes.bfloat16
def gentries(a):
    return np.ascontiguousarray(a.reshape(8, 16, -1).transpose(0, 2, 1)).reshape(8, -1)
def gtable(e):
    e = np.asarray(e); return np.ascontiguousarray(e.reshape(8, -1, 16).transpose(0, 2, 1)).reshape(128, -1).astype(np.int32)
XI, M, E, L, S, RO, D = 4096, 2048, 2048, 1024, 256, 3, 5
LB = 11
def forest(rng):
    o = np.argsort(rng.random((N, 8, M)), axis=-1); k = np.arange(M)
    inner = (2 * k + 2 < M) & (rng.random((N, 8, M)) >= 0.12); sw = rng.integers(0, 2, (N, 8, M))
    k0 = np.zeros_like(o); k1 = np.zeros_like(o)
    np.put_along_axis(k0, o, np.take_along_axis(o, np.where(inner, 2 * k + 1 + sw, k), 2), 2)
    np.put_along_axis(k1, o, np.take_along_axis(o, np.where(inner, 2 * k + 2 - sw, k), 2), 2)
    return o, k0, k1
def begin(rng, o, lo, hi):
    lv = rng.integers(lo, hi, (N, 8, L))
    return np.take_along_axis(o, 2 ** lv - 1 + (rng.random((N, 8, L)) * 2 ** lv).astype(np.int64), 2)
def vals(rng, n):
    return rng.integers(0, 256, (N, 8, 16, n))
def parts(rng):
    o, k0, k1 = forest(rng)
    return dict(o=o, x=vals(rng, XI), prev=rng.integers(0, XI, (N, 8, XI)), z=vals(rng, M), rs=vals(rng, M), kid0=k0, kid1=k1, env=vals(rng, E),
                start=begin(rng, o, LB - 3 - D, LB - 1), cur=rng.integers(0, XI, (N, 8, L)), w=rng.integers(1, 128, (N, 8, 16)), th=rng.integers(1000, 1500, (N, 8, 1)))
def pack(d):
    r = {}
    for k in ("x", "prev", "z", "rs", "kid0", "kid1", "env", "start", "cur", "w", "th"):
        if k in ("x", "z", "rs", "env"): r[k] = np.ascontiguousarray(d[k].reshape(N, 128, -1)).astype(np.float32).astype(BF)
        elif k in ("start", "cur"): r[k] = np.stack([gtable(a) for a in d[k]])
        elif k == "w": r[k] = d[k].reshape(N, 128, 1).astype(np.int32)
        else: r[k] = np.ascontiguousarray(d[k]).astype(np.int32)
    return r
def setup_inputs(rng):
    return pack(parts(rng))
def setup_inputs_full(rng):
    d = parts(rng)
    d["start"][:, ::2, :S] = d["o"][:, ::2, M // 2:M // 2 + S]; d["th"][:, ::2] = 0
    d["start"][::2, :, :S] = d["o"][::2, :, M // 2:M // 2 + S]; d["th"][::2] = 0
    return pack(d)
def setup_inputs_ties(rng):
    d = parts(rng)
    for k in ("x", "z", "rs", "env"): d[k] = d[k] // 64 * 64
    d["th"] = 64 * rng.integers(18, 22, (N, 8, 1))
    return pack(d)
def setup_inputs_alike(rng):
    d = parts(rng); m = np.arange(M)
    d["start"][:, 0] = d["o"][:, 0, M - 1:M]; d["th"][:, 0] = 0
    d["start"][:, 1] = rng.choice(np.array([0, M - 1]), (N, L)); d["cur"][:, 1] = rng.choice(np.array([0, XI - 1]), (N, L))
    d["prev"][:, 1] = np.where(rng.random((N, XI)) < 0.5, np.arange(XI), rng.choice(np.array([0, XI - 1]), (N, XI)))
    d["kid0"][:, 2] = (m + 1) & (M - 1); d["kid1"][:, 2] = (m + 1 + rng.integers(0, M - 1, (N, M))) & (M - 1)
    d["kid0"][:, 3] = m; d["kid1"][:, 3] = m
    d["start"][:, 3] = np.take_along_axis(rng.integers(0, M, (N, 40)), rng.integers(0, 40, (N, L)), 1)
    d["w"][:, 4] = 0; d["th"][:, 4] = 4096
    d["z"][:, 5] = 0; d["rs"][:, 5] = rng.choice(np.array([0, 255]), (N, 16, M))
    d["kid1"][:, 6] = d["kid0"][:, 6]; d["prev"][:, 6] = np.arange(XI)
    d["x"][:, 7] = 255; d["env"][:, 7] = 255; d["w"][:, 7] = 127; d["th"][:, 7] = 0
    return pack(d)
def setup_inputs_edges(rng):
    d = parts(rng); r = np.arange(N)[:, None]
    d["start"][:, :2, :S] = d["o"][:, :2, M // 2:M // 2 + S]; d["env"][:, :2] = 0
    c = rng.integers(0, 256, (16, 1)); d["x"][:, 0] = c
    d["rs"][:, 0] = np.where(rng.random((N, 1, M)) < 0.5, c, d["rs"][:, 0]); d["th"][:, 0] = r & 1
    c = 255 * rng.integers(0, 2, (16, 1)); d["x"][:, 1] = c
    d["rs"][:, 1] = 255 - c; d["rs"][:, 1, 0] = np.abs(255 - c[0] - rng.integers(0, 3, (N, M)))
    d["th"][:, 1] = np.array([4080, 4081, 4096, 4079])[r & 3]
    d["x"][:, 2:4] = rng.integers(250, 256, (N, 2, 16, XI)); d["w"][:, 2:4] = 127; d["env"][:, 3] = 0
    d["th"][:, 3] = rng.integers(2040, 2060, (N, 1))
    d["kid1"][:, 4] = np.where(rng.random((N, M)) < 0.5, d["kid0"][:, 4], d["kid1"][:, 4])
    return pack(d)
def setup_inputs_spread(rng):
    d = parts(rng); m = np.arange(M); lf = rng.random((N, 4, M)) < 0.5
    for k in ("kid0", "kid1"): d[k][:, 1::2] = np.where(lf, m, (m + rng.integers(1, M, (N, 4, M))) & (M - 1))
    for k, n in (("x", XI), ("z", M), ("rs", M), ("env", E)):
        d[k] = np.minimum((np.exp2(8 * rng.random((N, 8, 1, n))) * rng.random((N, 8, 16, n))).astype(np.int64), 255)
    d["w"] = np.minimum(np.exp2(7 * rng.random((N, 8, 16))).astype(np.int64), 127)
    d["th"] = np.minimum(np.exp2(12 * rng.random((N, 8, 1))).astype(np.int64), 4096); d["th"][:, 0] = 1; d["th"][:, 1] = 0
    d["start"] = begin(rng, d["o"], 0, LB)
    d["cur"] = np.minimum((XI * rng.random((N, 8, L)) ** 3).astype(np.int64), XI - 1)
    d["prev"] = np.where(rng.random((N, 8, XI)) < 0.5, np.maximum(np.arange(XI) - rng.integers(0, 40, (N, 8, XI)), 0), d["prev"])
    return pack(d)
def check_inputs(d):
    bad = []
    for k, lo, hi in (("x", 0, 255), ("prev", 0, XI - 1), ("z", 0, 255), ("rs", 0, 255), ("kid0", 0, M - 1), ("kid1", 0, M - 1), ("env", 0, 255), ("start", 0, M - 1), ("cur", 0, XI - 1), ("w", 0, 127), ("th", 0, 4096)):
        a = np.asarray(d[k]).astype(np.float32)
        if not np.all((a >= lo) & (a <= hi) & (a == np.floor(a))): bad.append("range of " + k)
    m = np.arange(M)
    if np.any((np.asarray(d["kid0"]) == m) != (np.asarray(d["kid1"]) == m)): bad.append("one kid of a node is the node itself, the other isn't")
    return bad
def pick(a, ix):
    return np.take_along_axis(a, ix[:, :, None, :], 3)
def reference(x, prev, z, rs, kid0, kid1, env, start, cur, w, th):
    def cols(a, more):
        b = a.astype(np.float32).astype(np.int32).reshape(N, 8, 16, -1)
        return np.concatenate([b, np.zeros((N, 8, 16, more), np.int32)], axis=3)
    X = cols(x, RO * L); Z = cols(z, 2 * S * RO); R = cols(rs, 2 * S * RO); EN = cols(env, 0)
    P = np.concatenate([prev.astype(np.int64), np.zeros((N, 8, RO * L), np.int64)], axis=2)
    own = np.zeros((N, 8, 1), np.int64) + np.arange(M, M + 2 * S * RO)
    K0 = np.concatenate([kid0.astype(np.int64), own], axis=2); K1 = np.concatenate([kid1.astype(np.int64), own], axis=2)
    F0 = np.stack([gentries(a) for a in start]).astype(np.int64); C = np.stack([gentries(a) for a in cur]).astype(np.int64)
    W = w.reshape(N, 8, 16, 1).astype(np.int32); TH = th.reshape(N, 8, 1).astype(np.int64)
    lower = np.arange(S)[None, :] < np.arange(S)[:, None]
    for t in range(RO):
        f = F0; s = C
        for step in range(D):
            k0 = np.take_along_axis(K0, f, 2); k1 = np.take_along_axis(K1, f, 2); go = k0 != f
            b = np.sum(pick(X, s) >= pick(Z, f), axis=2) >= 9
            f = np.where(go, np.where(b, k1, k0), f); s = np.where(go, np.take_along_axis(P, s, 2), s)
        xc = pick(X, C); rf = pick(R, f); a = np.sum(rf > xc, axis=2)
        y = pick(EN, (np.sum(W * xc, axis=2) + 97 * a) & (E - 1)); v = (xc + y) & 255
        fs = f[:, :, :S]; leaf = np.take_along_axis(K0, fs, 2) == fs
        first = ~np.any((fs[:, :, :, None] == fs[:, :, None, :]) & lower, axis=3)
        far = np.sum(np.abs(rf[..., :S] - v[..., :S]), axis=2) >= TH
        q, g, i = np.nonzero(leaf & first & far); at = fs[q, g, i]; n0 = M + 2 * S * t + 2 * i; xs = pick(X, s[:, :, :S])
        Z[q, g, :, at] = xs[q, g, :, i]; K0[q, g, at] = n0; K1[q, g, at] = n0 + 1
        R[q, g, :, n0] = rf[q, g, :, i]; R[q, g, :, n0 + 1] = (rf[q, g, :, i] + v[q, g, :, i]) >> 1
        came = np.roll(v, 1, axis=0)
        h = np.sum(W * came, axis=2) & (L - 1); lo = XI + L * t
        X[..., lo:lo + L] = came; P[..., lo:lo + L] = np.take_along_axis(C, h, 2)
        C = np.zeros((N, 8, 1), np.int64) + np.arange(lo, lo + L)
    return {"yk0": K0.astype(np.float32), "yk1": K1.astype(np.float32), "yr": np.ascontiguousarray(R[..., M:].reshape(N, 128, 2 * S * RO)).astype(np.float32).astype(BF), "yp": np.ascontiguousarray(P[..., XI:]).astype(np.float32)}

@@ -1,0 +1,570 @@
+import math
+from concourse.mybir import dt, AluOpType, AxisListType, ActivationFunctionType
+
+A = AluOpType
+AF = ActivationFunctionType
+NXP = 5 * 1024 + 256
+SCRATCH = {}
+
+
+def _sb(dtype, text):
+    for w in text.split():
+        n, c = w.split(":")
+        SCRATCH[n] = ("sbuf", [128, int(c)], dtype)
+
+
+_sb("bfloat16", "xs:4096 Pt:4096 Kt:4096 Zt:4096 Rt:3584 Et:2048 Ct:1024 XA:5376 XB:5376 XC:5376 XF:1024 VV:3072 Pg:1024 Kg:1024 "
+    "bt:1024 tm:1024 mm:1024 K5:256 Rd:512 aB:256 E:4096 qB:256 flB:256 winB:256 tK:256 xf:256 depB:256 ND:256 NDa:256 "
+    "NDb:256 NDt:768 ones:144 Q01:144 QP:144 QW:144 Q97:144 Q48:144 QS:144 Q1k:144 QK1:144 BD:128 BDs:128 BDf2:128 BDf1:128 "
+    "BDr:128 BD2:128 idB:128 idN:128 idH:128 idM:128 idMn:128 WK:8 dg:640 pg:512 cg:128 sfl:256 sfh:256")
+_sb("float32", "onesF:128 idF:128 BDF:128 bs:128 ts:128 hsS:64 thrR:256 i16:256 thx:256 laneL:16 dumpL:16 fd:16 fo:16 fp:16 "
+    "dO:16 e:16 col:64 thF:1 ypF:192 ykA:224 ykB:224 i16r:16 hF:64")
+_sb("int32", "prevI:256 k0I:128 k1I:128 curI:64 startI:64 wI:1 thI:1 pI:1 pmI:1 ownI:128 own2:128 ti:1024 tc:128 ix0:64 iy0:64 "
+    "hI:64 hJ:64 hK:64 hM:64 hN:64 yI:64 yJ:64 avI:256")
+_sb("uint16", "f0:64 fl:64 sl:384 hl:64 hp:64 el:64 fru:256 offU:16 depU:16")
+for _i in range(8):
+    SCRATCH["pb%d" % _i] = ("psum", [128, 512], "float32")
+
+NDMA = 40
+SEMAPHORES = ["sV", "sS", "sP", "sG", "loc"] + ["d%d" % i for i in range(NDMA)] + ["a%d%d" % (t, c) for t in range(3) for c in range(2)]
+
+
+def rank_program(g, core, T, topo):
+    rank = T.rank_of(core)
+    if rank is None:
+        return
+    dst = T.cores[(rank + 1) % len(T.cores)]
+    src = T.cores[(rank - 1) % len(T.cores)]
+
+    def pairs(a, b):
+        return topo.engines(a, b)[::2]
+
+    QUEUE = {"V": g.vector, "S": g.scalar, "P": g.tensor, "G": g, "D": g.sync}
+    SEM = {"V": "sV", "S": "sS", "P": "sP", "G": "sG"}
+    total = {}
+    seen = {}
+    recs = {}
+    ndma = [0]
+
+    def norm(r):
+        b = r[0]
+        if b.startswith("pb"):
+            return (b, 0, 512, None)
+        if len(r) == 1:
+            return (b, 0, SCRATCH[b][1][1], None)
+        if len(r) == 3:
+            return (b, r[1], r[2], None)
+        return r
+
+    def deps(q, isdma, reads, writes):
+        need = {}
+        for rs, w in ((reads, False), (writes, True)):
+            for r in rs:
+                b, lo, hi, tag = norm(r)
+                ps = b.startswith("pb")
+                for rec in recs.get(b, []):
+                    if rec[2] <= lo or rec[1] >= hi:
+                        continue
+                    if tag is not None and rec[3] is not None and tag != rec[3]:
+                        continue
+                    if not ps and not w and not rec[0]:
+                        continue
+                    if rec[6] == q and not isdma:
+                        if ps or w:
+                            continue
+                    need[rec[4]] = max(need.get(rec[4], 0), rec[5])
+        for s in need:
+            if seen.get((q, s), 0) < need[s]:
+                QUEUE[q].wait_ge(T.sem[s], need[s])
+                seen[(q, s)] = need[s]
+
+    def note(q, reads, writes, sem, val):
+        for r in reads:
+            b, lo, hi, tag = norm(r)
+            w = b.startswith("pb")
+            if w:
+                recs[b] = []
+            lst = recs.setdefault(b, [])
+            recs[b] = [x for x in lst if not ((not x[0]) and x[4] == sem and x[1] >= lo and x[2] <= hi and x[3] == tag)]
+            recs[b].append([w, lo, hi, tag, sem, val, q])
+        for r in writes:
+            b, lo, hi, tag = norm(r)
+            lst = recs.setdefault(b, [])
+            recs[b] = [x for x in lst if not (x[1] >= lo and x[2] <= hi and (tag is None or x[3] == tag))]
+            recs[b].append([True, lo, hi, tag, sem, val, q])
+
+    def op(q, calls, reads, writes):
+        deps(q, False, reads, writes)
+        s = SEM[q]
+        if not isinstance(calls, list):
+            calls = [calls]
+        for c in calls:
+            c().then_inc(T.sem[s], 1)
+            total[s] = total.get(s, 0) + 1
+        note(q, reads, writes, s, total[s])
+
+    def dma(q, out, in_, reads, writes):
+        deps(q, True, reads, writes)
+        s = "d%d" % ndma[0]
+        ndma[0] += 1
+        QUEUE[q].dma_start(out, in_).then_inc(T.sem[s], 16)
+        total[s] = 16
+        note(q + "dma", reads, writes, s, 16)
+
+    def cp(out, in_, rd, wr):
+        op("V", lambda: g.vector.tensor_copy(out=out, in_=in_), rd, wr)
+
+    def tt(out, a, b, o, rd, wr):
+        op("V", lambda: g.vector.tensor_tensor(out=out, in0=a, in1=b, op=o), rd, wr)
+
+    def ts(out, a, s1, o1, rd, wr, s2=None, o2=None):
+        if o2 is None:
+            op("V", lambda: g.vector.tensor_scalar(out=out, in0=a, scalar1=s1, scalar2=None, op0=o1), rd, wr)
+        else:
+            op("V", lambda: g.vector.tensor_scalar(out=out, in0=a, scalar1=s1, scalar2=s2, op0=o1, op1=o2), rd, wr)
+
+    def act(out, in_, rd, wr, func=AF.Copy, **kw):
+        op("S", lambda: g.scalar.activation(out=out, in_=in_, func=func, **kw), rd, wr)
+
+    def mm(out, l, r, st, sp):
+        return lambda: g.tensor.matmul(out, l, r, st, sp)
+
+    def direct(bank, col, n, Q, data, base, rd, stop=True):
+        b = T[bank]
+        op("P", [mm(b[:, col:col + n], Q[:, 15 - r:143 - r], data[:, base + r:base + 16 * n:16], r == 0, stop and r == 15)
+                 for r in range(16)], rd, [(bank,)])
+
+    def block(bank, col, n, Q, data, rd):
+        b = T[bank]
+        op("P", [mm(b[:, col:col + n], Q[:, 15 - r:143 - r], data[:, n * r:n * r + n], r == 0, r == 15) for r in range(16)],
+           rd, [(bank,)])
+
+    dma("D", T.k0I[:, :], T.kid0[:, :], [], [("k0I",)])
+    dma("D", T.k1I[:, :], T.kid1[:, :], [], [("k1I",)])
+    dma("S", T.startI[:, :], T.start[:, :], [], [("startI",)])
+    dma("S", T.curI[:, :], T.cur[:, :], [], [("curI",)])
+    dma("D", T.prevI[:, :], T.prev[:, :], [], [("prevI",)])
+    dma("S", T.wI[:, :], T.w[:, :], [], [("wI",)])
+    dma("D", T.xs[:, :], T.x[:, :], [], [("xs",)])
+    dma("S", T.Zt[:, 0:2048], T.z[:, :], [], [("Zt", 0, 2048)])
+
+    V = g.vector
+    op("V", lambda: V.memset(T.ones[:, :], 1.0), [], [("ones",)])
+    op("V", lambda: V.memset(T.onesF[:, :], 1.0), [], [("onesF",)])
+    op("V", lambda: V.memset(T.thI[:, :], 0), [], [("thI",)])
+    op("V", lambda: V.memset(T.Zt[:, 2048:4096], 0.0), [], [("Zt", 2048, 4096)])
+    op("V", lambda: V.memset(T.Kt[:, :], 0.0), [], [("Kt",)])
+    ZU = ("Zt", 2048, 4096)
+    act(T.Pt[:, 0:2048], T.Zt[:, 2048:4096], [ZU], [("Pt", 0, 2048)])
+    act(T.Pt[:, 2048:4096], T.Zt[:, 2048:4096], [ZU], [("Pt", 2048, 4096)])
+
+    def iota(name, lo, hi, pattern, base, cm, small):
+        ap = T[name][:, lo:hi]
+        if small:
+            op("G", lambda: g.iota(ap, pattern, base, cm, allow_small_or_imprecise_dtypes=True), [], [(name, lo, hi)])
+        else:
+            op("G", lambda: g.iota(ap, pattern, base, cm), [], [(name, lo, hi)])
+
+    def sel(out, in_, pattern, cmp, base, cm, n, rd, wr):
+        op("G", lambda: g.affine_select(out[:, 0:n], in_[:, 0:n], pattern, cmp, 0.0, base, cm), rd, wr)
+
+    iota("pI", 0, 1, [[0, 1]], 0, 1, False)
+    iota("i16r", 0, 16, [[1, 16]], 0, 0, True)
+    iota("ownI", 0, 128, [[1, 128]], 0, 128, False)
+    sel(T.Q01, T.ones, [[0, 9], [1, 16]], A.is_equal, -15, 0, 144, [("ones",)], [("Q01",)])
+    sel(T.Q01, T.Q01, [[-16, 9], [0, 16]], A.is_ge, 0, 1, 144, [("Q01",)], [("Q01",)])
+    sel(T.Q01, T.Q01, [[16, 9], [0, 16]], A.is_ge, 15, -1, 144, [("Q01",)], [("Q01",)])
+    sel(T.idF, T.onesF, [[-1, 128]], A.is_equal, 0, 1, 128, [("onesF",)], [("idF",)])
+    sel(T.BD, T.ones, [[-16, 8], [0, 16]], A.is_ge, 0, 1, 128, [("ones",)], [("BD",)])
+    sel(T.BD, T.BD, [[16, 8], [0, 16]], A.is_ge, 15, -1, 128, [("BD",)], [("BD",)])
+    iota("sfl", 0, 256, [[1, 256]], 0, 0, True)
+    iota("laneL", 0, 16, [[16, 16]], 0, 0, True)
+    iota("i16", 0, 256, [[0, 16], [1, 16]], 0, 0, True)
+    iota("NDa", 0, 256, [[0, 2], [2, 128]], 0, 0, True)
+    iota("NDb", 0, 256, [[1, 2], [0, 128]], 0, 0, True)
+
+    ts(T.own2[:, :], T.ownI[:, :], 2047, A.bitwise_and, [("ownI",)], [("own2",)])
+
+    def digits(di, src, n, tmp, to, out, oo):
+        for j, (o, v) in enumerate(((A.bitwise_and, 255), (A.arith_shift_right, 8))):
+            a, b = to + j * n, oo + j * n
+            ts(T[tmp][:, a:a + n], T[src][:, :], v, o, [(src,)], [(tmp, a, a + n)])
+            cp(T[out][:, b:b + n], T[tmp][:, a:a + n], [(tmp, a, a + n)], [(out, b, b + n)])
+
+    digits(0, "k0I", 128, "ti", 0, "dg", 0)
+    digits(2, "k1I", 128, "ti", 256, "dg", 256)
+    tt(T.dg[:, 512:640], T.k0I[:, :], T.own2[:, :], A.not_equal, [("k0I",), ("own2",)], [("dg", 512, 640)])
+    for i, j in ((0, 0), (1, 1), (2, 2), (3, 3), (6, 4)):
+        dma("D", T.Kt[i:128:16, 0:2048], T.dg[:, 128 * j:128 * j + 128], [("dg", 128 * j, 128 * j + 128)], [("Kt", 0, 2048, "r%d" % i)])
+    cp(T.f0[:, :], T.startI[:, :], [("startI",)], [("f0",)])
+    cp(T.sl[:, 0:64], T.curI[:, :], [("curI",)], [("sl", 0, 64)])
+    digits(0, "prevI", 256, "ti", 512, "pg", 0)
+    dma("D", T.Pt[0:128:16, :], T.pg[:, 0:256], [("pg", 0, 256)], [("Pt", 0, 4096, "r0")])
+    dma("D", T.Pt[1:128:16, :], T.pg[:, 256:512], [("pg", 256, 512)], [("Pt", 0, 4096, "r1")])
+    dma("D", T.thI[0:128:16, :], T.th[:, :], [], [("thI",)])
+    ts(T.pmI[:, :], T.pI[:, :], 15, A.bitwise_and, [("pI",)], [("pmI",)])
+    C = {}
+    ncol = [0]
+
+    def column(nm):
+        i = ncol[0]
+        ncol[0] += 1
+        C[nm] = (T.col[:, i:i + 1], ("col", i, i + 1))
+        return C[nm]
+
+    pm, pmr = column("pm")
+    cp(pm, T.pmI[:, :], [("pmI",)], [pmr])
+    wc, wcr = column("w")
+    cp(wc, T.wI[:, :], [("wI",)], [wcr])
+    ts(T.e[:, :], T.i16r[:, :], pm, A.is_equal, [("i16r",), pmr], [("e",)])
+
+    def E1(j):
+        return T.e[:, j:j + 1]
+
+    def colop(nm, a, s1, o1, s2, o2, rd):
+        c, r = column(nm)
+        ts(c, a, s1, o1, rd, [r], s2, o2)
+        return c, r
+
+    kw0, kw0r = colop("kw0", E1(1), 256.0, A.mult, E1(0), A.add, [("e",)])
+    kw1, kw1r = colop("kw1", E1(3), 256.0, A.mult, E1(2), A.add, [("e",)])
+    kdk, kdkr = colop("kdk", kw1, kw0, A.subtract, None, None, [kw1r, kw0r])
+    er = ("e",)
+
+    def scaled(name, src, c, rd):
+        act(T[name][:, :], src, rd, [(name,)], scale=c)
+
+    W1 = T.Q01[:, 15:128:16]
+    scaled("WK", W1, kdk, [("Q01",), kdkr])
+    scaled("QP", T.Q01[:, :], kw0, [("Q01",), kw0r])
+    scaled("BDf1", T.BD[:, :], E1(6), [("BD",), er])
+    scaled("QW", T.Q01[:, :], wc, [("Q01",), wcr])
+    dma("D", T.Rt[:, 0:2048], T.rs[:, :], [], [("Rt", 0, 2048)])
+    dma("D", T.Et[:, :], T.env[:, :], [], [("Et",)])
+    dma("D", T.Kt[4:128:16, :], T.sfl[:, :], [("sfl",)], [("Kt", 0, 4096, "r4")])
+
+    def late1():
+        act(T.Rt[:, 2048:3584], T.Pt[:, 0:1536], [("Pt", 0, 2048)], [("Rt", 2048, 3584)], scale=0.0)
+        act(T.Ct[:, :], T.Pt[:, 0:1024], [("Pt", 0, 2048)], [("Ct",)], scale=0.0)
+        act(T.sfh[:, :], T.sfl[:, :], [("sfl",), pmr], [("sfh",)], func=AF.Identity, scale=0.0, bias=pm)
+        dma("D", T.Kt[5:128:16, :], T.sfh[:, :], [("sfh",)], [("Kt", 0, 4096, "r5")])
+        for i in range(4):
+            dma("D", T.Kt[i:128:16, 2048:4096], T.Kt[4 + i % 2:128:16, 2048:4096], [("Kt", 2048, 4096, "r%d" % (4 + i % 2))],
+                [("Kt", 2048, 4096, "r%d" % i)])
+
+    def late2():
+        kse, kser = colop("kse", E1(5), 256.0, A.mult, E1(4), A.add, [er])
+        m13, m13r = colop("m13", E1(1), E1(3), A.add, None, None, [er])
+        m02, m02r = colop("m02", E1(0), E1(2), A.add, None, None, [er])
+        ca, car = colop("ca", m13, 8.0, A.mult, E1(2), A.add, [er, m13r])
+        cb, cbr = colop("cb", ca, E1(6), A.add, None, None, [er, car])
+        ra, rar = colop("ra", E1(4), -1.0, A.mult, E1(5), A.subtract, [er])
+        rm, rmr = colop("rowm", ra, 1.0, A.add, None, None, [rar])
+        rn, rnr = colop("rown", rm, -1.0, A.mult, None, None, [rmr])
+        f2, f2r = colop("f2", E1(6), 2.0, A.mult, None, None, [er])
+        q1, q1r = colop("q1", E1(0), 1024.0, A.mult, None, None, [er])
+        pw, pwr = column("pw")
+        act(pw, pm, [pmr], [pwr], func=AF.Exp, scale=-math.log(2.0))
+        act(T.thrR[:, :], T.i16[:, :], [("i16",)], [("thrR",)], func=AF.Exp, scale=-math.log(2.0))
+        scaled("BDr", T.BD[:, :], pw, [("BD",), pwr])
+        scaled("BDs", T.BD[:, :], kse, [("BD",), kser])
+        scaled("BDf2", T.BD[:, :], f2, [("BD",), f2r])
+        scaled("BD2", T.BD[:, :], 2.0, [("BD",)])
+        scaled("Q97", T.Q01[:, :], 97.0, [("Q01",)])
+        scaled("Q48", T.Q01[:, :], 48.5, [("Q01",)])
+        scaled("QS", T.Q01[:, :], E1(0), [("Q01",), er])
+        scaled("Q1k", T.Q01[:, :], q1, [("Q01",), q1r])
+        scaled("idB", T.idF[:, :], 1.0, [("idF",)])
+        scaled("idN", T.idF[:, :], -1.0, [("idF",)])
+        scaled("idH", T.idF[:, :], 0.5, [("idF",)])
+        scaled("idM", T.idF[:, :], rm, [("idF",), rmr])
+        scaled("idMn", T.idF[:, :], rn, [("idF",), rnr])
+        scaled("QK1", T.Q01[:, :], kw1, [("Q01",), kw1r])
+
+    def late3():
+        m13, m13r = C["m13"]
+        m02, m02r = C["m02"]
+        cb, cbr = C["cb"]
+        ts(T.NDb[:, :], T.NDb[:, :], m13, A.mult, [("NDb",), m13r], [("NDb",)])
+        ts(T.NDa[:, :], T.NDa[:, :], m02, A.mult, [("NDa",), m02r, cbr], [("NDa",)], cb, A.add)
+        tt(T.ND[:, :], T.NDa[:, :], T.NDb[:, :], A.add, [("NDa",), ("NDb",)], [("ND",)])
+        for t in range(3):
+            c, r = colop("c%d" % t, m13, 2.0 * t, A.mult, None, None, [m13r])
+            ts(T.NDt[:, 256 * t:256 * t + 256], T.ND[:, :], c, A.add, [("ND",), r], [("NDt", 256 * t, 256 * t + 256)])
+        ts(T.thrR[:, :], T.thrR[:, :], 2.5, A.mult, [("thrR",)], [("thrR",)])
+        cp(T.BDF[:, :], T.BD[:, :], [("BD",)], [("BDF",)])
+        cp(T.thF[:, :], T.thI[:, :], [("thI",)], [("thF",)])
+        op("P", mm(T.pb4[:, 100:101], T.BDF[:, :], T.thF[:, :], True, True), [("BDF",), ("thF",)], [("pb4",)])
+        colop("thm", T.pb4[:, 100:101], -1048576.0, A.add, None, None, [("pb4",)])
+        ts(T.laneL[:, :], T.laneL[:, :], pm, A.add, [("laneL",), pmr], [("laneL",)])
+        ts(T.dumpL[:, :], T.laneL[:, :], 3584.0, A.add, [("laneL",)], [("dumpL",)])
+
+    def late4():
+        ts(T.Et[:, :], T.Et[:, :], -256.0, A.add, [("Et",)], [("Et",)])
+        digits(0, "curI", 64, "tc", 0, "cg", 0)
+        dma("D", T.Ct[0:128:16, :], T.cg[:, 0:64], [("cg", 0, 64)], [("Ct", 0, 1024, "r0")])
+        dma("D", T.Ct[1:128:16, :], T.cg[:, 64:128], [("cg", 64, 128)], [("Ct", 0, 1024, "r1")])
+
+    XP = ["XA", "XB", "XC", "XF"]
+
+    def nodes(h, k):
+        nm = "f0" if k == 0 else "fl"
+        return T[nm][:, 32 * h:32 * h + 32], (nm, 32 * h, 32 * h + 32)
+
+    def kid(h, k):
+        l, r = nodes(h, k)
+        act(T.Kg[:, 512 * h:512 * h + 512], T.Kt[:, :].indirect(l), [("Kt",), r], [("Kg", 512 * h, 512 * h + 512)])
+
+    def cmpz(t, h, k):
+        l, r = nodes(h, k)
+        a = 1024 * k + 512 * h
+        tt(T.bt[:, 512 * h:512 * h + 512], T.Zt[:, :].indirect(l), T[XP[t]][:, a:a + 512], A.is_le,
+           [("Zt",), r, (XP[t], a, a + 512)], [("bt", 512 * h, 512 * h + 512)])
+
+    def pediff(h):
+        op("P", [mm(T.pb0[32 * h:32 * h + 32, r:128:16], T.Kg[:, 512 * h + r:512 * h + 512:16], T.WK[:, :], True, True) for r in range(16)],
+           [("Kg", 512 * h, 512 * h + 512), ("WK",)], [("pb0",)])
+
+    def pecnt(h):
+        op("P", [mm(T.pb6[32 * h:32 * h + 32, r:128:16], T.bt[:, 512 * h + r:512 * h + 512:16], W1, True, True) for r in range(16)],
+           [("bt", 512 * h, 512 * h + 512), ("Q01",)], [("pb6",)])
+
+    def gather(eng, out, outr, win, winr, lst, lstr):
+        if eng == "S":
+            act(out, win.indirect(lst), [winr, lstr], [outr])
+        else:
+            cp(out, win.indirect(lst), [winr, lstr], [outr])
+
+    def xg(eng, t, k, a, b):
+        o = 1024 * k
+        out, outr = T[XP[t]][:, o + a:o + b], (XP[t], o + a, o + b)
+        if t == 0:
+            lo, hi = 64 * k + a // 16, 64 * k + b // 16
+            gather(eng, out, outr, T.xs[:, :], ("xs",), T.sl[:, lo:hi], ("sl", lo, hi))
+        else:
+            w = 1024 * (k - 1)
+            gather(eng, out, outr, T[XP[t - 1]][:, w:w + 1024], (XP[t - 1], w, w + 1024), T.hl[:, a // 16:b // 16], ("hl", a // 16, b // 16))
+
+    def pgat(k, n):
+        gather("S", T.Pg[:, 0:n], ("Pg",), T.Pt[:, :], ("Pt",), T.sl[:, 64 * k:64 * k + n // 16], ("sl", 64 * k, 64 * k + n // 16))
+        direct("pb2", 0, n // 16, T.QP, T.Pg, 0, [("Pg",), ("QP",)])
+
+    def plist(k, n):
+        cp(T.sl[:, 64 * k:64 * k + n // 16], T.pb2[:, 0:n // 16], [("pb2",)], [("sl", 64 * k, 64 * k + n // 16)])
+
+    def hsum(t, h):
+        direct("pb2", 64 + 32 * h, 32, T.QW, T[XP[t]], 512 * h, [(XP[t], 512 * h, 512 * h + 512), ("QW",)])
+
+    def hcopy():
+        ts(T.hsS[:, 0:32], T.pb2[:, 64:96], 776.0, A.add, [("pb2",)], [("hsS", 0, 32)])
+        cp(T.hsS[:, 32:64], T.pb2[:, 96:128], [("pb2",)], [("hsS", 32, 64)])
+
+    def hlist():
+        cp(T.hI[:, :], T.pb2[:, 64:128], [("pb2",)], [("hI",)])
+        ts(T.hJ[:, :], T.hI[:, :], 1023, A.bitwise_and, [("hI",)], [("hJ",)])
+        cp(T.hl[:, :], T.hJ[:, :], [("hJ",)], [("hl",)])
+
+    def arrived(t, h):
+        s = "a%d%d" % (t, h)
+        total[s] = len(pairs(src, core))
+        recs.setdefault(XP[t + 1], []).append([True, 512 * h, 512 * h + 512, None, s, total[s], "remote"])
+
+    def send(t, h):
+        a, b = 1024 * t + 512 * h, 1024 * t + 512 * h + 512
+        deps("G", True, [("VV", a, b)], [])
+        en = pairs(core, dst)
+        mask = sum(1 << x for x in en)
+        rid, pid, _ = topo.addr(dst)
+        g.remote_dma(out_ap=T[XP[t + 1]][:, 512 * h:512 * h + 512], in_ap=T.VV[:, a:b], remote_sem=T.sem["a%d%d" % (t, h)],
+                     local_sem=T.sem.loc, pid=pid, routing_id=rid, dma_engine_mask=mask)
+        total["loc"] = total.get("loc", 0) + len(en)
+
+    def outcome(t, h):
+        a, b = 512 * h, 512 * h + 512
+        tt(T.tm[:, a:b], T.Et[:, :].indirect(T.el[:, 32 * h:32 * h + 32]), T[XP[t]][:, a:b], A.add,
+           [("Et",), ("el",), (XP[t], a, b)], [("tm", a, b)])
+        ts(T.mm[:, a:b], T.tm[:, a:b], 0.0, A.is_lt, [("tm", a, b)], [("mm", a, b)], 256.0, A.mult)
+        op("P", [mm(T.pb7[:, :], T.idB[:, :], T.tm[:, a:b], True, False), mm(T.pb7[:, :], T.idB[:, :], T.mm[:, a:b], False, True)],
+           [("tm", a, b), ("mm", a, b), ("idB",)], [("pb7",)])
+        act(T.VV[:, 1024 * t + a:1024 * t + b], T.pb7[:, :], [("pb7",)], [("VV", 1024 * t + a, 1024 * t + b)])
+        send(t, h)
+
+    def eqs():
+        for c in range(16):
+            n = 256 - 16 * c
+            ts(T.E[:, 256 * c:256 * c + n], T.fru[:, 16 * c:256], T.pb1[:, c:c + 1], A.is_equal, [("fru",), ("pb1",)],
+               [("E", 256 * c, 256 * c + n)])
+        d = T.pb5
+        ms = [mm(d[:, 0:256], T.BDr[:, :], T.E[:, 0:256], True, False), mm(d[:, 16:256], T.BD2[:, :], T.E[:, 16:256], False, False)]
+        for c in range(1, 16):
+            if c < 15:
+                ms.append(mm(d[:, 16 * c + 16:256], T.BD2[:, :], T.E[:, 256 * c + 16:256 * c + 256 - 16 * c], False, False))
+            ms.append(mm(d[:, 16 * c:16 * c + 16], T.BDr[:, :], T.E[:, 256 * c:256 * c + 16], False, c == 15))
+        op("P", ms, [("E",), ("BDr",), ("BD2",)], [("pb5",)])
+
+    def rwrites1(t):
+        a = 1024 * t
+        op("P", [mm(T.pb7[:, 0:256], T.idH[:, :], T.Rd[:, 0:256], True, False), mm(T.pb7[:, 0:256], T.idH[:, :], T.VV[:, a:a + 256], False, True)],
+           [("Rd",), ("VV", a, a + 256), ("idH",)], [("pb7",)])
+        n = 2048 + 512 * t
+        tt(T.Rt[:, n:n + 512:2], T.Rd[:, 0:256], T.winB[:, :], A.mult, [("Rd",), ("winB",)], [("Rt", n, n + 512, "even")])
+
+    def rwrites2(t):
+        n = 2048 + 512 * t
+        ts(T.avI[:, :], T.pb7[:, 0:256], -0.25, A.add, [("pb7",)], [("avI",)])
+        tt(T.Rt[:, n + 1:n + 512:2], T.avI[:, :], T.winB[:, :], A.mult, [("avI",), ("winB",)], [("Rt", n, n + 512, "odd")])
+
+    def ypn(t, xn):
+        block("pb2", 128, 64, T.QW, T[xn], [(xn, 0, 1024), ("QW",)])
+        cp(T.yI[:, :], T.pb2[:, 128:192], [("pb2",)], [("yI",)])
+        ts(T.yJ[:, :], T.yI[:, :], 1023, A.bitwise_and, [("yI",)], [("yJ",)])
+        ts(T.ypF[:, 64 * t:64 * t + 64], T.yJ[:, :], float(4096 + 1024 * (t - 1)), A.add, [("yJ",)], [("ypF", 64 * t, 64 * t + 64)])
+        dma("D", T.yp[:, 1024 * t:1024 * t + 1024], T.ypF[:, 64 * t:64 * t + 64], [("ypF", 64 * t, 64 * t + 64)], [])
+
+    def yp0a():
+        ts(T.hK[:, :], T.hJ[:, :], 15, A.bitwise_and, [("hJ",)], [("hK",)])
+        ts(T.hM[:, :], T.hJ[:, :], 4, A.arith_shift_right, [("hJ",)], [("hM",)])
+        ts(T.hN[:, :], T.hK[:, :], 64.0, A.mult, [("hK",)], [("hN",)])
+        tt(T.hF[:, :], T.hN[:, :], T.hM[:, :], A.add, [("hN",), ("hM",)], [("hF",)])
+        cp(T.hp[:, :], T.hF[:, :], [("hF",)], [("hp",)])
+
+    def yp0b():
+        gather("S", T.Pg[:, :], ("Pg",), T.Ct[:, :], ("Ct",), T.hp[:, :], ("hp",))
+        block("pb2", 0, 64, T.QP, T.Pg, [("Pg",), ("QP",)])
+
+    def yp0c():
+        cp(T.ypF[:, 0:64], T.pb2[:, 0:64], [("pb2",)], [("ypF", 0, 64)])
+        dma("D", T.yp[:, 0:1024], T.ypF[:, 0:64], [("ypF", 0, 64)], [])
+
+    for t in range(3):
+        XT = XP[t]
+        if t == 0:
+            xg("S", 0, 0, 0, 512)
+            xg("V", 0, 0, 512, 1024)
+        for k in range(5):
+            kid(0, k)
+            cmpz(t, 0, k)
+            pediff(0)
+            op("P", mm(T.pb3[:, 0:256], T.BDf1[:, :], T.Kg[:, 0:256], k == 0, k == 4), [("Kg", 0, 256), ("BDf1",)], [("pb3",)])
+            if t > 0 and k == 0:
+                hsum(t, 0)
+            pecnt(0)
+            if t == 0 and k > 0:
+                plist(k + 1, 1024 if k < 4 else 256)
+            kid(1, k)
+            if t == 0 and k == 0:
+                pgat(0, 1024)
+                late1()
+            cmpz(t, 1, k)
+            if t > 0 and k == 0:
+                hsum(t, 1)
+            pecnt(1)
+            pediff(1)
+            direct("pb1", 0, 64, T.QP, T.Kg, 0, [("Kg",), ("QP",)], stop=False)
+            if k == 0:
+                if t == 0:
+                    plist(1, 1024)
+                else:
+                    hlist()
+            if t == 0 and k < 4:
+                if k < 3:
+                    pgat(k + 1, 1024)
+                else:
+                    pgat(4, 256)
+                xg("V", 0, k + 1, 256, 1024)
+                xg("S", 0, k + 1, 0, 256)
+                if k == 1:
+                    late2()
+                if k == 2:
+                    late3()
+                if k == 3:
+                    late4()
+            elif k < 4:
+                xg("V", t, k + 1, 768, 1024)
+                xg("S", t, k + 1, 0, 768)
+                if t == 1 and k == 2:
+                    yp0b()
+            elif t < 2:
+                xg("S", t, 5, 0, 256)
+            if t == 1 and k == 4:
+                yp0c()
+            ts(T.bs[0:64, :], T.pb6[0:64, 0:128], 8.5, A.is_ge, [("pb6",)], [("bs",)])
+            tt(T.ts[0:64, :], T.pb0[0:64, 0:128], T.bs[0:64, :], A.mult, [("pb0",), ("bs",)], [("ts",)])
+            op("P", mm(T.pb1[:, 0:64], T.ts[0:64, :], T.idF[0:64, 0:64], False, True), [("ts",), ("idF",)], [("pb1",)])
+            if t > 0:
+                if k == 0:
+                    hcopy()
+                if k == 1:
+                    rwrites1(t - 1)
+                if k == 2:
+                    rwrites2(t - 1)
+                if t == 1 and k == 1:
+                    yp0a()
+                if t == 2 and k == 3:
+                    ypn(1, "XC")
+            elif k == 4:
+                hsum(0, 0)
+                hsum(0, 1)
+                hcopy()
+            cp(T.fl[:, :], T.pb1[:, 0:64], [("pb1",)], [("fl",)])
+        l0, l1 = ("fl", 0, 32), ("fl", 32, 64)
+        gather("S", T.K5[:, :], ("K5",), T.Kt[:, :], ("Kt",), T.fl[:, 0:16], l0)
+        tt(T.bt[:, 512:1024], T.Rt[:, :].indirect(T.fl[:, 32:64]), T[XT][:, 512:1024], A.is_gt, [("Rt",), l1, (XT, 512, 1024)], [("bt", 512, 1024)])
+        gather("S", T.Rd[:, :], ("Rd",), T.Rt[:, :], ("Rt",), T.fl[:, 0:32], l0)
+        op("P", [mm(T.pb4[:, 0:256], T.BDs[:, :], T.K5[:, :], True, True), mm(T.pb4[:, 256:512], T.BDf2[:, :], T.K5[:, :], True, True)],
+           [("K5",), ("BDs",), ("BDf2",)], [("pb4",)])
+        direct("pb6", 32, 32, T.Q97, T.bt, 512, [("bt", 512, 1024), ("Q97",)])
+        cp(T.fru[:, :], T.pb4[:, 0:256], [("pb4",)], [("fru",)])
+        op("P", [mm(T.pb7[:, :], T.idB[:, :], T.Rd[:, :], True, False), mm(T.pb7[:, :], T.idN[:, :], T[XT][:, 0:512], False, True)],
+           [("Rd",), (XT, 0, 512), ("idB",), ("idN",)], [("pb7",)])
+        if t < 2:
+            act(T.depB[:, :], T.pb3[:, 0:256], [("pb3",)], [("depB",)])
+        act(T.bt[:, 0:512], T.pb7[:, :], [("pb7",), C["neg"][1]] if "neg" in C else [("pb7",)], [("bt", 0, 512)], func=AF.Sign, bias=-0.5)
+        direct("pb6", 0, 32, T.Q48, T.bt, 0, [("bt", 0, 512), ("Q48",)])
+        eqs()
+        if t < 2:
+            direct("pb2", 0, 16, T.Q1k, T.depB, 0, [("depB",), ("Q1k",)])
+        tt(T.ix0[:, :], T.pb6[:, 0:64], T.hsS[:, :], A.add, [("pb6",), ("hsS",)], [("ix0",)])
+        ts(T.iy0[:, :], T.ix0[:, :], 2047, A.bitwise_and, [("ix0",)], [("iy0",)])
+        cp(T.el[:, :], T.iy0[:, :], [("iy0",)], [("el",)])
+        outcome(t, 0)
+        op("P", [mm(T.pb3[:, 0:256], T.idM[:, :], T.NDt[:, 256 * t:256 * t + 256], True, False), mm(T.pb3[:, 0:256], T.idMn[:, :], T.K5[:, :], False, True)],
+           [("idM",), ("idMn",), ("NDt",), ("K5",)], [("pb3",)])
+        v0 = ("VV", 1024 * t, 1024 * t + 256)
+        op("P", [mm(T.pb0[:, 0:256], T.idB[:, :], T.Rd[:, 0:256], True, False), mm(T.pb0[:, 0:256], T.idN[:, :], T.VV[:, 1024 * t:1024 * t + 256], False, True)],
+           [("Rd",), v0, ("idB",), ("idN",)], [("pb0",)])
+        act(T.aB[:, :], T.pb0[:, 0:256], [("pb0",)], [("aB",)], func=AF.Abs)
+        outcome(t, 1)
+        tt(T.qB[:, :], T.pb5[:, 0:256], T.thrR[:, :], A.is_ge, [("pb5",), ("thrR",)], [("qB",)])
+        tt(T.flB[:, :], T.pb4[:, 256:512], T.qB[:, :], A.is_equal, [("pb4",), ("qB",)], [("flB",)])
+        op("P", mm(T.pb5[:, 256:512], T.BD[:, :], T.aB[:, :], True, True), [("aB",), ("BD",)], [("pb5",)])
+        direct("pb6", 64, 16, T.QS, T.flB, 0, [("flB",), ("QS",)])
+        ts(T.thx[:, :], T.flB[:, :], C["thm"][0], A.mult, [("flB",), C["thm"][1]], [("thx",)], 1048576.0, A.add)
+        if t < 2:
+            tt(T.dO[:, :], T.pb2[:, 0:16], T.laneL[:, :], A.add, [("pb2",), ("laneL",)], [("dO",)])
+            cp(T.depU[:, :], T.dO[:, :], [("dO",)], [("depU",)])
+            gather("S", T.xf[:, :], ("xf",), T[XT][:, 0:NXP], (XT, 0, NXP), T.depU[:, :], ("depU",))
+        tt(T.fd[:, :], T.pb1[:, 0:16], T.dumpL[:, :], A.subtract, [("pb1",), ("dumpL",)], [("fd",)])
+        tt(T.winB[:, :], T.pb5[:, 256:512], T.thx[:, :], A.is_ge, [("pb5",), ("thx",)], [("winB",)])
+        tt(T.fo[:, :], T.pb6[:, 64:80], T.fd[:, :], A.mult, [("pb6",), ("fd",)], [("fo",)])
+        tt(T.fp[:, :], T.fo[:, :], T.dumpL[:, :], A.add, [("fo",), ("dumpL",)], [("fp",)])
+        tt(T.tK[:, :], T.pb3[:, 0:256], T.winB[:, :], A.mult, [("pb3",), ("winB",)], [("tK",)])
+        cp(T.offU[:, :], T.fp[:, :], [("fp",)], [("offU",)])
+        tt(T.Kt[:, :].indirect(T.offU[:, :]), T.K5[:, :], T.tK[:, :], A.add, [("K5",), ("tK",), ("offU",)], [("Kt",)])
+        if t < 2:
+            cp(T.Zt[:, :].indirect(T.offU[:, :]), T.xf[:, :], [("xf",), ("offU",)], [("Zt",)])
+        arrived(t, 0)
+        arrived(t, 1)
+    block("pb3", 0, 224, T.QP, T.Kt, [("Kt",), ("QP",)])
+    act(T.ykA[:, :], T.pb3[:, 0:224], [("pb3",)], [("ykA",)])
+    dma("D", T.yk0[:, :], T.ykA[:, :], [("ykA",)], [])
+    rwrites1(2)
+    rwrites2(2)
+    dma("D", T.yr[:, :], T.Rt[:, 2048:3584], [("Rt", 2048, 3584)], [])
+    block("pb4", 0, 224, T.QK1, T.Kt, [("Kt",), ("QK1",)])
+    act(T.ykB[:, :], T.pb4[:, 0:224], [("pb4",)], [("ykB",)])
+    dma("D", T.yk1[:, :], T.ykB[:, :], [("ykB",)], [])
+    ypn(2, "XF")
+    for s in total:
+        if seen.get(("G", s), 0) < total[s]:
+            g.wait_ge(T.sem[s], total[s])

@@ -3,6 +3,9 @@ from concourse.mybir import dt, AluOpType, AxisListType, ActivationFunctionType
 
 A = AluOpType
 AF = ActivationFunctionType
+NE = 4
+NS0 = (64, 320, 320, 1024)
+NS1 = 800
 NXP = 5 * 1024 + 256
 SCRATCH = {}
 
@@ -14,13 +17,13 @@ def _sb(dtype, text):
 
 
 _sb("bfloat16", "xs:4096 Pt:4096 Kt:4096 Zt:4096 Rt:3584 Et:2048 Ct:1024 XA:5376 XB:5376 XC:5376 XF:1024 VV:3072 Pg:1024 Kg:1024 "
-    "bt:1024 tm:1024 mm:1024 K5:256 Rd:512 aB:256 E:4096 qB:256 flB:256 winB:256 tK:256 xf:256 depB:256 ND:256 NDa:256 "
-    "NDb:256 NDt:768 ones:144 Q01:144 QP:144 QW:144 Q97:144 Q48:144 QS:144 Q1k:144 QK1:144 BD:128 BDs:128 BDf2:128 BDf1:128 "
-    "BDr:128 BD2:128 idB:128 idN:128 idH:128 idM:128 idMn:128 WK:8 dg:640 pg:512 cg:128 sfl:256 sfh:256")
-_sb("float32", "onesF:128 idF:128 BDF:128 bs:128 ts:128 hsS:64 thrR:256 i16:256 thx:256 laneL:16 dumpL:16 fd:16 fo:16 fp:16 "
-    "dO:16 e:16 col:64 thF:1 ypF:192 ykA:224 ykB:224 i16r:16 hF:64")
-_sb("int32", "prevI:256 k0I:128 k1I:128 curI:64 startI:64 wI:1 thI:1 pI:1 pmI:1 ownI:128 own2:128 ti:1024 tc:128 ix0:64 iy0:64 "
-    "hI:64 hJ:64 hK:64 hM:64 hN:64 yI:64 yJ:64 avI:256")
+    "bt:1024 tm:1024 mm:1024 K5:256 Rg:256 aB:256 E:4096 qB:256 flB:256 winB:256 tK:256 xf:256 depB:256 NDa:256 NDc:256 "
+    "NDe:256 NDt:768 ones:144 zer:144 Q01:144 QP:144 QW:144 Q97:144 Q48:144 QS:144 Q1k:144 QKK:144 BD:128 BDs:128 BDf2:128 "
+    "BDf1:128 idB:128 idN:128 idH:128 idS:128 idMn:128 DM:512 WK:16 dg:640 pg:512 cg:128 sfl:256 sfh:256 sfi:256")
+_sb("float32", "onesF:128 idF:128 BDF:128 bs:128 ts:128 F:128 w16:16 hsS:64 thrR:256 thx:256 laneL:16 dumpL:16 fd:16 fo:16 fp:16 "
+    "dO:16 col:16 thF:1 ypF:192 ykA:224 ykB:224 hF:64")
+_sb("int32", "prevI:256 k0I:128 k1I:128 curI:64 startI:64 wI:1 thI:1 pI:1 pmI:1 pnI:1 ownI:128 own2:128 ti:1024 tc:128 ix0:64 "
+    "iy0:64 yA:224 yB:224 yC:224 hI:64 hJ:64 hK:64 hM:64 hN:64 yI:64 yJ:64 avI:256")
 _sb("uint16", "f0:64 fl:64 sl:384 hl:64 hp:64 el:64 fru:256 offU:16 depU:16")
 for _i in range(8):
     SCRATCH["pb%d" % _i] = ("psum", [128, 512], "float32")
@@ -111,52 +114,44 @@ def rank_program(g, core, T, topo):
         total[s] = 16
         note(q + "dma", reads, writes, s, 16)
 
+    V = g.vector
+
     def cp(out, in_, rd, wr):
-        op("V", lambda: g.vector.tensor_copy(out=out, in_=in_), rd, wr)
+        op("V", lambda: V.tensor_copy(out=out, in_=in_), rd, wr)
 
     def tt(out, a, b, o, rd, wr):
-        op("V", lambda: g.vector.tensor_tensor(out=out, in0=a, in1=b, op=o), rd, wr)
+        op("V", lambda: V.tensor_tensor(out=out, in0=a, in1=b, op=o), rd, wr)
 
     def ts(out, a, s1, o1, rd, wr, s2=None, o2=None):
         if o2 is None:
-            op("V", lambda: g.vector.tensor_scalar(out=out, in0=a, scalar1=s1, scalar2=None, op0=o1), rd, wr)
+            op("V", lambda: V.tensor_scalar(out=out, in0=a, scalar1=s1, scalar2=None, op0=o1), rd, wr)
         else:
-            op("V", lambda: g.vector.tensor_scalar(out=out, in0=a, scalar1=s1, scalar2=s2, op0=o1, op1=o2), rd, wr)
+            op("V", lambda: V.tensor_scalar(out=out, in0=a, scalar1=s1, scalar2=s2, op0=o1, op1=o2), rd, wr)
+
+    def fill(name, lo, hi, v):
+        op("V", lambda: V.memset(T[name][:, lo:hi], v), [], [(name, lo, hi)])
 
     def act(out, in_, rd, wr, func=AF.Copy, **kw):
         op("S", lambda: g.scalar.activation(out=out, in_=in_, func=func, **kw), rd, wr)
 
+    def gather(eng, out, outr, win, winr, lst, lstr):
+        if eng == "S":
+            act(out, win.indirect(lst), [winr, lstr], [outr])
+        else:
+            cp(out, win.indirect(lst), [winr, lstr], [outr])
+
     def mm(out, l, r, st, sp):
         return lambda: g.tensor.matmul(out, l, r, st, sp)
 
-    def direct(bank, col, n, Q, data, base, rd, stop=True):
+    def direct(bank, col, n, Q, data, base, rd):
         b = T[bank]
-        op("P", [mm(b[:, col:col + n], Q[:, 15 - r:143 - r], data[:, base + r:base + 16 * n:16], r == 0, stop and r == 15)
+        op("P", [mm(b[:, col:col + n], Q[:, 15 - r:143 - r], data[:, base + r:base + 16 * n:16], r == 0, r == 15)
                  for r in range(16)], rd, [(bank,)])
 
     def block(bank, col, n, Q, data, rd):
         b = T[bank]
         op("P", [mm(b[:, col:col + n], Q[:, 15 - r:143 - r], data[:, n * r:n * r + n], r == 0, r == 15) for r in range(16)],
            rd, [(bank,)])
-
-    dma("D", T.k0I[:, :], T.kid0[:, :], [], [("k0I",)])
-    dma("D", T.k1I[:, :], T.kid1[:, :], [], [("k1I",)])
-    dma("S", T.startI[:, :], T.start[:, :], [], [("startI",)])
-    dma("S", T.curI[:, :], T.cur[:, :], [], [("curI",)])
-    dma("D", T.prevI[:, :], T.prev[:, :], [], [("prevI",)])
-    dma("S", T.wI[:, :], T.w[:, :], [], [("wI",)])
-    dma("D", T.xs[:, :], T.x[:, :], [], [("xs",)])
-    dma("S", T.Zt[:, 0:2048], T.z[:, :], [], [("Zt", 0, 2048)])
-
-    V = g.vector
-    op("V", lambda: V.memset(T.ones[:, :], 1.0), [], [("ones",)])
-    op("V", lambda: V.memset(T.onesF[:, :], 1.0), [], [("onesF",)])
-    op("V", lambda: V.memset(T.thI[:, :], 0), [], [("thI",)])
-    op("V", lambda: V.memset(T.Zt[:, 2048:4096], 0.0), [], [("Zt", 2048, 4096)])
-    op("V", lambda: V.memset(T.Kt[:, :], 0.0), [], [("Kt",)])
-    ZU = ("Zt", 2048, 4096)
-    act(T.Pt[:, 0:2048], T.Zt[:, 2048:4096], [ZU], [("Pt", 0, 2048)])
-    act(T.Pt[:, 2048:4096], T.Zt[:, 2048:4096], [ZU], [("Pt", 2048, 4096)])
 
     def iota(name, lo, hi, pattern, base, cm, small):
         ap = T[name][:, lo:hi]
@@ -165,143 +160,148 @@ def rank_program(g, core, T, topo):
         else:
             op("G", lambda: g.iota(ap, pattern, base, cm), [], [(name, lo, hi)])
 
-    def sel(out, in_, pattern, cmp, base, cm, n, rd, wr):
-        op("G", lambda: g.affine_select(out[:, 0:n], in_[:, 0:n], pattern, cmp, 0.0, base, cm), rd, wr)
+    def sel(name, src, pattern, cmp, base, cm, n):
+        op("G", lambda: g.affine_select(T[name][:, 0:n], T[src][:, 0:n], pattern, cmp, 0.0, base, cm), [(src, 0, n)], [(name, 0, n)])
 
-    iota("pI", 0, 1, [[0, 1]], 0, 1, False)
-    iota("i16r", 0, 16, [[1, 16]], 0, 0, True)
-    iota("ownI", 0, 128, [[1, 128]], 0, 128, False)
-    sel(T.Q01, T.ones, [[0, 9], [1, 16]], A.is_equal, -15, 0, 144, [("ones",)], [("Q01",)])
-    sel(T.Q01, T.Q01, [[-16, 9], [0, 16]], A.is_ge, 0, 1, 144, [("Q01",)], [("Q01",)])
-    sel(T.Q01, T.Q01, [[16, 9], [0, 16]], A.is_ge, 15, -1, 144, [("Q01",)], [("Q01",)])
-    sel(T.idF, T.onesF, [[-1, 128]], A.is_equal, 0, 1, 128, [("onesF",)], [("idF",)])
-    sel(T.BD, T.ones, [[-16, 8], [0, 16]], A.is_ge, 0, 1, 128, [("ones",)], [("BD",)])
-    sel(T.BD, T.BD, [[16, 8], [0, 16]], A.is_ge, 15, -1, 128, [("BD",)], [("BD",)])
-    iota("sfl", 0, 256, [[1, 256]], 0, 0, True)
-    iota("laneL", 0, 16, [[16, 16]], 0, 0, True)
-    iota("i16", 0, 256, [[0, 16], [1, 16]], 0, 0, True)
-    iota("NDa", 0, 256, [[0, 2], [2, 128]], 0, 0, True)
-    iota("NDb", 0, 256, [[1, 2], [0, 128]], 0, 0, True)
+    def put(name, n, pattern, entries, lo=0):
+        for j, (base, v) in enumerate(entries):
+            ap, r = (T.zer[:, 0:n], ("zer",)) if j == 0 else (T[name][:, lo:lo + n], (name, lo, lo + n))
+            op("G", lambda ap=ap, base=base, v=v: g.affine_select(T[name][:, lo:lo + n], ap, pattern, A.not_equal, float(v), base, 1),
+               [r], [(name, lo, lo + n)])
 
-    ts(T.own2[:, :], T.ownI[:, :], 2047, A.bitwise_and, [("ownI",)], [("own2",)])
+    def putQ(name, entries):
+        put(name, 144, [[-16, 9], [1000, 16]], [(-15000 - i, v) for i, v in entries])
 
-    def digits(di, src, n, tmp, to, out, oo):
-        for j, (o, v) in enumerate(((A.bitwise_and, 255), (A.arith_shift_right, 8))):
-            a, b = to + j * n, oo + j * n
-            ts(T[tmp][:, a:a + n], T[src][:, :], v, o, [(src,)], [(tmp, a, a + n)])
-            cp(T[out][:, b:b + n], T[tmp][:, a:a + n], [(tmp, a, a + n)], [(out, b, b + n)])
+    def putB(name, entries):
+        put(name, 128, [[-16, 8], [0, 16]], [(-i, v) for i, v in entries])
 
-    digits(0, "k0I", 128, "ti", 0, "dg", 0)
-    digits(2, "k1I", 128, "ti", 256, "dg", 256)
-    tt(T.dg[:, 512:640], T.k0I[:, :], T.own2[:, :], A.not_equal, [("k0I",), ("own2",)], [("dg", 512, 640)])
-    for i, j in ((0, 0), (1, 1), (2, 2), (3, 3), (6, 4)):
-        dma("D", T.Kt[i:128:16, 0:2048], T.dg[:, 128 * j:128 * j + 128], [("dg", 128 * j, 128 * j + 128)], [("Kt", 0, 2048, "r%d" % i)])
-    cp(T.f0[:, :], T.startI[:, :], [("startI",)], [("f0",)])
-    cp(T.sl[:, 0:64], T.curI[:, :], [("curI",)], [("sl", 0, 64)])
-    digits(0, "prevI", 256, "ti", 512, "pg", 0)
-    dma("D", T.Pt[0:128:16, :], T.pg[:, 0:256], [("pg", 0, 256)], [("Pt", 0, 4096, "r0")])
-    dma("D", T.Pt[1:128:16, :], T.pg[:, 256:512], [("pg", 256, 512)], [("Pt", 0, 4096, "r1")])
-    dma("D", T.thI[0:128:16, :], T.th[:, :], [], [("thI",)])
-    ts(T.pmI[:, :], T.pI[:, :], 15, A.bitwise_and, [("pI",)], [("pmI",)])
+    def putD(name, lo, places, v=1.0):
+        put(name, 128, [[-16, 8], [999, 16]], [(-1000 * i, v) for i in places], lo)
+
     C = {}
-    ncol = [0]
 
     def column(nm):
-        i = ncol[0]
-        ncol[0] += 1
+        i = len(C)
         C[nm] = (T.col[:, i:i + 1], ("col", i, i + 1))
         return C[nm]
 
+    dma("D", T.prevI[:, :], T.prev[:, :], [], [("prevI",)])
+    dma("D", T.k0I[:, :], T.kid0[:, :], [], [("k0I",)])
+    dma("S", T.curI[:, :], T.cur[:, :], [], [("curI",)])
+    dma("S", T.startI[:, :], T.start[:, :], [], [("startI",)])
+    dma("D", T.k1I[:, :], T.kid1[:, :], [], [("k1I",)])
+    dma("S", T.wI[:, :], T.w[:, :], [], [("wI",)])
+    dma("D", T.xs[:, :], T.x[:, :], [], [("xs",)])
+    dma("S", T.Zt[:, 0:2048], T.z[:, :], [], [("Zt", 0, 2048)])
+
+    iota("pI", 0, 1, [[0, 1]], 0, 1, False)
+    iota("sfl", 0, 256, [[1, 256]], 0, 0, True)
+    iota("ownI", 0, 128, [[1, 128]], 0, 128, False)
     pm, pmr = column("pm")
+    pe, per = column("pe")
+    fill("ones", 0, 144, 1.0)
+    fill("onesF", 0, 128, 1.0)
+    ts(T.pmI[:, :], T.pI[:, :], 15, A.bitwise_and, [("pI",)], [("pmI",)])
+    ts(T.pnI[:, :], T.pI[:, :], 7, A.bitwise_and, [("pI",)], [("pnI",)])
+    fill("thI", 0, 1, 0)
     cp(pm, T.pmI[:, :], [("pmI",)], [pmr])
-    wc, wcr = column("w")
-    cp(wc, T.wI[:, :], [("wI",)], [wcr])
-    ts(T.e[:, :], T.i16r[:, :], pm, A.is_equal, [("i16r",), pmr], [("e",)])
+    ts(pe, T.pnI[:, :], 8.0, A.add, [("pnI",)], [per])
+    fill("Zt", 2048, 4096, 0.0)
+    fill("Kt", 0, 4096, 0.0)
+    fill("zer", 0, 144, 0.0)
+    ZU = ("Zt", 2048, 4096)
+    act(T.sfh[:, :], T.sfl[:, :], [("sfl",), pmr], [("sfh",)], func=AF.Identity, scale=0.0, bias=pm)
+    act(T.sfi[:, :], T.sfl[:, :], [("sfl",), per], [("sfi",)], func=AF.Identity, scale=0.0, bias=pe)
+    act(T.Pt[:, 0:2048], T.Zt[:, 2048:4096], [ZU], [("Pt", 0, 2048)])
+    act(T.Pt[:, 2048:4096], T.Zt[:, 2048:4096], [ZU], [("Pt", 2048, 4096)])
 
-    def E1(j):
-        return T.e[:, j:j + 1]
+    sel("Q01", "ones", [[0, 9], [1, 16]], A.is_equal, -15, 0, 144)
+    sel("Q01", "Q01", [[-16, 9], [0, 16]], A.is_ge, 0, 1, 144)
+    sel("Q01", "Q01", [[16, 9], [0, 16]], A.is_ge, 15, -1, 144)
+    putQ("QP", [(0, 1), (1, 256)])
+    put("WK", 8, [[-16, 8]], [(0, 1), (-1, 256)], 0)
+    put("WK", 8, [[-16, 8]], [(0, -1), (-1, -256), (-2, 1), (-3, 256)], 8)
+    putB("BDf1", [(6, 1)])
+    sel("idF", "onesF", [[-1, 128]], A.is_equal, 0, 1, 128)
+    sel("BD", "ones", [[-16, 8], [0, 16]], A.is_ge, 0, 1, 128)
+    sel("BD", "BD", [[16, 8], [0, 16]], A.is_ge, 15, -1, 128)
+    iota("laneL", 0, 16, [[16, 16]], 0, 0, True)
+    for nm, v in (("idB", 1.0), ("idN", -1.0), ("idH", 0.5), ("idS", -128.0)):
+        put(nm, 128, [[-1, 128]], [(0, v)])
+    putB("BDs", [(4, 1), (5, 256)])
+    putB("BDf2", [(6, 2)])
+    putQ("Q1k", [(0, 1024)])
+    putQ("QS", [(0, 1)])
+    iota("NDa", 0, 256, [[0, 2], [2, 128]], 0, 0, True)
+    iota("NDc", 0, 256, [[0, 2], [2, 128]], 1, 0, True)
+    iota("NDe", 0, 256, [[0, 256]], 1, 0, True)
+    for t in range(3):
+        iota("NDt", 256 * t, 256 * t + 256, [[1, 2], [0, 128]], 8 + 2 * t, 0, True)
+    putD("DM", 0, (0,))
+    putD("DM", 128, (2,))
+    putD("DM", 256, (1, 3))
+    putD("DM", 384, (6,))
+    putD("idMn", 0, (0, 1, 2, 3, 6), -1.0)
+    putQ("QKK", [(0, 1), (1, 256), (2, 4096), (3, 1048576)])
 
-    def colop(nm, a, s1, o1, s2, o2, rd):
-        c, r = column(nm)
-        ts(c, a, s1, o1, rd, [r], s2, o2)
-        return c, r
+    def digits(name, n, tmp, to, out, oo):
+        for j, (o, v) in enumerate(((A.bitwise_and, 255), (A.arith_shift_right, 8))):
+            a, b = to + j * n, oo + j * n
+            ts(T[tmp][:, a:a + n], T[name][:, :], v, o, [(name,)], [(tmp, a, a + n)])
+            cp(T[out][:, b:b + n], T[tmp][:, a:a + n], [(tmp, a, a + n)], [(out, b, b + n)])
 
-    kw0, kw0r = colop("kw0", E1(1), 256.0, A.mult, E1(0), A.add, [("e",)])
-    kw1, kw1r = colop("kw1", E1(3), 256.0, A.mult, E1(2), A.add, [("e",)])
-    kdk, kdkr = colop("kdk", kw1, kw0, A.subtract, None, None, [kw1r, kw0r])
-    er = ("e",)
-
-    def scaled(name, src, c, rd):
-        act(T[name][:, :], src, rd, [(name,)], scale=c)
-
-    W1 = T.Q01[:, 15:128:16]
-    scaled("WK", W1, kdk, [("Q01",), kdkr])
-    scaled("QP", T.Q01[:, :], kw0, [("Q01",), kw0r])
-    scaled("BDf1", T.BD[:, :], E1(6), [("BD",), er])
-    scaled("QW", T.Q01[:, :], wc, [("Q01",), wcr])
+    cp(T.f0[:, :], T.startI[:, :], [("startI",)], [("f0",)])
+    cp(T.sl[:, 0:64], T.curI[:, :], [("curI",)], [("sl", 0, 64)])
+    digits("prevI", 256, "ti", 512, "pg", 0)
+    dma("D", T.Pt[0:128:16, :], T.pg[:, 0:256], [("pg", 0, 256)], [("Pt", 0, 4096, "r0")])
+    dma("D", T.Pt[1:128:16, :], T.pg[:, 256:512], [("pg", 256, 512)], [("Pt", 0, 4096, "r1")])
+    ts(T.own2[:, :], T.ownI[:, :], 2047, A.bitwise_and, [("ownI",)], [("own2",)])
+    digits("k0I", 128, "ti", 0, "dg", 0)
+    digits("k1I", 128, "ti", 256, "dg", 256)
+    tt(T.dg[:, 512:640], T.k0I[:, :], T.own2[:, :], A.not_equal, [("k0I",), ("own2",)], [("dg", 512, 640)])
+    dma("D", T.Kt[4:128:16, :], T.sfl[:, :], [("sfl",)], [("Kt", 0, 4096, "r4")])
+    dma("D", T.Kt[5:128:16, :], T.sfh[:, :], [("sfh",)], [("Kt", 0, 4096, "r5")])
+    for i in range(4):
+        nm = ("sfl", "sfi")[i % 2]
+        dma("D", T.Kt[i:128:16, 2048:4096], T[nm][0:64, :], [(nm,)], [("Kt", 2048, 4096, "r%d" % i)])
+    for i, j in ((0, 0), (1, 1), (2, 2), (3, 3), (6, 4)):
+        dma("D", T.Kt[i:128:16, 0:2048], T.dg[:, 128 * j:128 * j + 128], [("dg", 128 * j, 128 * j + 128)], [("Kt", 0, 2048, "r%d" % i)])
+    dma("D", T.thI[0:128:16, :], T.th[:, :], [], [("thI",)])
     dma("D", T.Rt[:, 0:2048], T.rs[:, :], [], [("Rt", 0, 2048)])
     dma("D", T.Et[:, :], T.env[:, :], [], [("Et",)])
-    dma("D", T.Kt[4:128:16, :], T.sfl[:, :], [("sfl",)], [("Kt", 0, 4096, "r4")])
+    wc, wcr = column("w")
+    cp(wc, T.wI[:, :], [("wI",)], [wcr])
+    W1 = T.Q01[:, 15:128:16]
+
+    def scaled(name, c, rd):
+        ts(T[name][:, :], T.Q01[:, :], c, A.mult, [("Q01",)] + rd, [(name,)])
+
+    LN = math.log(1.85)
 
     def late1():
-        act(T.Rt[:, 2048:3584], T.Pt[:, 0:1536], [("Pt", 0, 2048)], [("Rt", 2048, 3584)], scale=0.0)
-        act(T.Ct[:, :], T.Pt[:, 0:1024], [("Pt", 0, 2048)], [("Ct",)], scale=0.0)
-        act(T.sfh[:, :], T.sfl[:, :], [("sfl",), pmr], [("sfh",)], func=AF.Identity, scale=0.0, bias=pm)
-        dma("D", T.Kt[5:128:16, :], T.sfh[:, :], [("sfh",)], [("Kt", 0, 4096, "r5")])
-        for i in range(4):
-            dma("D", T.Kt[i:128:16, 2048:4096], T.Kt[4 + i % 2:128:16, 2048:4096], [("Kt", 2048, 4096, "r%d" % (4 + i % 2))],
-                [("Kt", 2048, 4096, "r%d" % i)])
+        fill("Rt", 2048, 3584, 0.0)
+        fill("Ct", 0, 1024, 0.0)
+        scaled("QW", wc, [wcr])
+
+    def late1b():
+        ts(T.laneL[:, :], T.laneL[:, :], pm, A.add, [("laneL",), pmr], [("laneL",)])
+        scaled("Q97", 97.0, [])
+        scaled("Q48", 48.5, [])
+        ts(T.dumpL[:, :], T.laneL[:, :], 3584.0, A.add, [("laneL",)], [("dumpL",)])
 
     def late2():
-        kse, kser = colop("kse", E1(5), 256.0, A.mult, E1(4), A.add, [er])
-        m13, m13r = colop("m13", E1(1), E1(3), A.add, None, None, [er])
-        m02, m02r = colop("m02", E1(0), E1(2), A.add, None, None, [er])
-        ca, car = colop("ca", m13, 8.0, A.mult, E1(2), A.add, [er, m13r])
-        cb, cbr = colop("cb", ca, E1(6), A.add, None, None, [er, car])
-        ra, rar = colop("ra", E1(4), -1.0, A.mult, E1(5), A.subtract, [er])
-        rm, rmr = colop("rowm", ra, 1.0, A.add, None, None, [rar])
-        rn, rnr = colop("rown", rm, -1.0, A.mult, None, None, [rmr])
-        f2, f2r = colop("f2", E1(6), 2.0, A.mult, None, None, [er])
-        q1, q1r = colop("q1", E1(0), 1024.0, A.mult, None, None, [er])
-        pw, pwr = column("pw")
-        act(pw, pm, [pmr], [pwr], func=AF.Exp, scale=-math.log(2.0))
-        act(T.thrR[:, :], T.i16[:, :], [("i16",)], [("thrR",)], func=AF.Exp, scale=-math.log(2.0))
-        scaled("BDr", T.BD[:, :], pw, [("BD",), pwr])
-        scaled("BDs", T.BD[:, :], kse, [("BD",), kser])
-        scaled("BDf2", T.BD[:, :], f2, [("BD",), f2r])
-        scaled("BD2", T.BD[:, :], 2.0, [("BD",)])
-        scaled("Q97", T.Q01[:, :], 97.0, [("Q01",)])
-        scaled("Q48", T.Q01[:, :], 48.5, [("Q01",)])
-        scaled("QS", T.Q01[:, :], E1(0), [("Q01",), er])
-        scaled("Q1k", T.Q01[:, :], q1, [("Q01",), q1r])
-        scaled("idB", T.idF[:, :], 1.0, [("idF",)])
-        scaled("idN", T.idF[:, :], -1.0, [("idF",)])
-        scaled("idH", T.idF[:, :], 0.5, [("idF",)])
-        scaled("idM", T.idF[:, :], rm, [("idF",), rmr])
-        scaled("idMn", T.idF[:, :], rn, [("idF",), rnr])
-        scaled("QK1", T.Q01[:, :], kw1, [("Q01",), kw1r])
+        act(T.w16[:, :], T.laneL[:, :], [("laneL",)], [("w16",)], func=AF.Exp, scale=-LN, bias=128 * LN)
+        act(T.thrR[:, :], T.sfl[:, :], [("sfl",)], [("thrR",)], func=AF.Exp, scale=-LN, bias=128 * LN + math.log(2.5))
 
     def late3():
-        m13, m13r = C["m13"]
-        m02, m02r = C["m02"]
-        cb, cbr = C["cb"]
-        ts(T.NDb[:, :], T.NDb[:, :], m13, A.mult, [("NDb",), m13r], [("NDb",)])
-        ts(T.NDa[:, :], T.NDa[:, :], m02, A.mult, [("NDa",), m02r, cbr], [("NDa",)], cb, A.add)
-        tt(T.ND[:, :], T.NDa[:, :], T.NDb[:, :], A.add, [("NDa",), ("NDb",)], [("ND",)])
-        for t in range(3):
-            c, r = colop("c%d" % t, m13, 2.0 * t, A.mult, None, None, [m13r])
-            ts(T.NDt[:, 256 * t:256 * t + 256], T.ND[:, :], c, A.add, [("ND",), r], [("NDt", 256 * t, 256 * t + 256)])
-        ts(T.thrR[:, :], T.thrR[:, :], 2.5, A.mult, [("thrR",)], [("thrR",)])
         cp(T.BDF[:, :], T.BD[:, :], [("BD",)], [("BDF",)])
         cp(T.thF[:, :], T.thI[:, :], [("thI",)], [("thF",)])
         op("P", mm(T.pb4[:, 100:101], T.BDF[:, :], T.thF[:, :], True, True), [("BDF",), ("thF",)], [("pb4",)])
-        colop("thm", T.pb4[:, 100:101], -1048576.0, A.add, None, None, [("pb4",)])
-        ts(T.laneL[:, :], T.laneL[:, :], pm, A.add, [("laneL",), pmr], [("laneL",)])
-        ts(T.dumpL[:, :], T.laneL[:, :], 3584.0, A.add, [("laneL",)], [("dumpL",)])
+        c, r = column("thm")
+        ts(c, T.pb4[:, 100:101], -1048576.0, A.add, [("pb4",)], [r])
 
     def late4():
-        ts(T.Et[:, :], T.Et[:, :], -256.0, A.add, [("Et",)], [("Et",)])
-        digits(0, "curI", 64, "tc", 0, "cg", 0)
+        digits("curI", 64, "tc", 0, "cg", 0)
         dma("D", T.Ct[0:128:16, :], T.cg[:, 0:64], [("cg", 0, 64)], [("Ct", 0, 1024, "r0")])
         dma("D", T.Ct[1:128:16, :], T.cg[:, 64:128], [("cg", 64, 128)], [("Ct", 0, 1024, "r1")])
 
@@ -321,19 +321,13 @@ def rank_program(g, core, T, topo):
         tt(T.bt[:, 512 * h:512 * h + 512], T.Zt[:, :].indirect(l), T[XP[t]][:, a:a + 512], A.is_le,
            [("Zt",), r, (XP[t], a, a + 512)], [("bt", 512 * h, 512 * h + 512)])
 
-    def pediff(h):
-        op("P", [mm(T.pb0[32 * h:32 * h + 32, r:128:16], T.Kg[:, 512 * h + r:512 * h + 512:16], T.WK[:, :], True, True) for r in range(16)],
+    def pekids(h):
+        op("P", [mm(T.pb0[32 * h:32 * h + 32, r:256:16], T.Kg[:, 512 * h + r:512 * h + 512:16], T.WK[:, :], True, True) for r in range(16)],
            [("Kg", 512 * h, 512 * h + 512), ("WK",)], [("pb0",)])
 
     def pecnt(h):
         op("P", [mm(T.pb6[32 * h:32 * h + 32, r:128:16], T.bt[:, 512 * h + r:512 * h + 512:16], W1, True, True) for r in range(16)],
            [("bt", 512 * h, 512 * h + 512), ("Q01",)], [("pb6",)])
-
-    def gather(eng, out, outr, win, winr, lst, lstr):
-        if eng == "S":
-            act(out, win.indirect(lst), [winr, lstr], [outr])
-        else:
-            cp(out, win.indirect(lst), [winr, lstr], [outr])
 
     def xg(eng, t, k, a, b):
         o = 1024 * k
@@ -347,6 +341,8 @@ def rank_program(g, core, T, topo):
 
     def pgat(k, n):
         gather("S", T.Pg[:, 0:n], ("Pg",), T.Pt[:, :], ("Pt",), T.sl[:, 64 * k:64 * k + n // 16], ("sl", 64 * k, 64 * k + n // 16))
+
+    def psum(n):
         direct("pb2", 0, n // 16, T.QP, T.Pg, 0, [("Pg",), ("QP",)])
 
     def plist(k, n):
@@ -355,13 +351,17 @@ def rank_program(g, core, T, topo):
     def hsum(t, h):
         direct("pb2", 64 + 32 * h, 32, T.QW, T[XP[t]], 512 * h, [(XP[t], 512 * h, 512 * h + 512), ("QW",)])
 
-    def hcopy():
-        ts(T.hsS[:, 0:32], T.pb2[:, 64:96], 776.0, A.add, [("pb2",)], [("hsS", 0, 32)])
-        cp(T.hsS[:, 32:64], T.pb2[:, 96:128], [("pb2",)], [("hsS", 32, 64)])
+    def hlow():
+        ts(T.hsS[:, 0:16], T.pb2[:, 64:80], 776.0, A.add, [("pb2",)], [("hsS", 0, 16)])
+
+    def hhigh():
+        cp(T.hsS[:, 16:64], T.pb2[:, 80:128], [("pb2",)], [("hsS", 16, 64)])
 
     def hlist():
         cp(T.hI[:, :], T.pb2[:, 64:128], [("pb2",)], [("hI",)])
+        hlow()
         ts(T.hJ[:, :], T.hI[:, :], 1023, A.bitwise_and, [("hI",)], [("hJ",)])
+        hhigh()
         cp(T.hl[:, :], T.hJ[:, :], [("hJ",)], [("hl",)])
 
     def arrived(t, h):
@@ -379,35 +379,49 @@ def rank_program(g, core, T, topo):
                      local_sem=T.sem.loc, pid=pid, routing_id=rid, dma_engine_mask=mask)
         total["loc"] = total.get("loc", 0) + len(en)
 
-    def outcome(t, h):
-        a, b = 512 * h, 512 * h + 512
-        tt(T.tm[:, a:b], T.Et[:, :].indirect(T.el[:, 32 * h:32 * h + 32]), T[XP[t]][:, a:b], A.add,
-           [("Et",), ("el",), (XP[t], a, b)], [("tm", a, b)])
-        ts(T.mm[:, a:b], T.tm[:, a:b], 0.0, A.is_lt, [("tm", a, b)], [("mm", a, b)], 256.0, A.mult)
-        op("P", [mm(T.pb7[:, :], T.idB[:, :], T.tm[:, a:b], True, False), mm(T.pb7[:, :], T.idB[:, :], T.mm[:, a:b], False, True)],
-           [("tm", a, b), ("mm", a, b), ("idB",)], [("pb7",)])
-        act(T.VV[:, 1024 * t + a:1024 * t + b], T.pb7[:, :], [("pb7",)], [("VV", 1024 * t + a, 1024 * t + b)])
-        send(t, h)
+    def out0(t):
+        tt(T.tm[:, 0:512], T.Et[:, :].indirect(T.el[:, 0:32]), T[XP[t]][:, 0:512], A.add,
+           [("Et",), ("el",), (XP[t], 0, 512)], [("tm", 0, 512)])
+        ts(T.mm[:, 0:512], T.tm[:, 0:512], 0.0, A.is_lt, [("tm", 0, 512)], [("mm", 0, 512)], 256.0, A.mult)
+        op("P", [mm(T.pb7[:, :], T.idB[:, :], T.tm[:, 0:512], True, False), mm(T.pb7[:, :], T.idB[:, :], T.mm[:, 0:512], False, True)],
+           [("tm", 0, 512), ("mm", 0, 512), ("idB",)], [("pb7",)])
 
-    def eqs():
-        for c in range(16):
+    def out0c(t):
+        act(T.VV[:, 1024 * t:1024 * t + 512], T.pb7[:, :], [("pb7",)], [("VV", 1024 * t, 1024 * t + 512)])
+        send(t, 0)
+
+    def sums1(t, bank, stop):
+        op("P", [mm(T[bank][:, :], T.idB[:, :], T.tm[:, 512:1024], True, False),
+                 mm(T[bank][:, :], T.idB[:, :], T[XP[t]][:, 512:1024], False, stop)],
+           [("tm", 512, 1024), (XP[t], 512, 1024), ("idB",)], [(bank,)])
+
+    def out1a(t):
+        gather("S", T.tm[:, 512:1024], ("tm", 512, 1024), T.Et[:, :], ("Et",), T.el[:, 32:64], ("el",))
+        sums1(t, "pb3", True)
+
+    def out1b():
+        act(T.mm[:, 512:1024], T.pb3[:, :], [("pb3",)], [("mm", 512, 1024)], func=AF.Sign, bias=0.5)
+
+    def out1c(t):
+        op("P", mm(T.pb0[:, :], T.idS[:, :], T.mm[:, 512:1024], False, True), [("mm", 512, 1024), ("idS",)], [("pb0",)])
+        act(T.VV[:, 1024 * t + 512:1024 * t + 1024], T.pb0[:, :], [("pb0",)], [("VV", 1024 * t + 512, 1024 * t + 1024)], bias=128.0)
+        send(t, 1)
+
+    def eqs(c0, c1):
+        ms = []
+        for c in range(c0, c1):
             n = 256 - 16 * c
-            ts(T.E[:, 256 * c:256 * c + n], T.fru[:, 16 * c:256], T.pb1[:, c:c + 1], A.is_equal, [("fru",), ("pb1",)],
-               [("E", 256 * c, 256 * c + n)])
-        d = T.pb5
-        ms = [mm(d[:, 0:256], T.BDr[:, :], T.E[:, 0:256], True, False), mm(d[:, 16:256], T.BD2[:, :], T.E[:, 16:256], False, False)]
-        for c in range(1, 16):
-            if c < 15:
-                ms.append(mm(d[:, 16 * c + 16:256], T.BD2[:, :], T.E[:, 256 * c + 16:256 * c + 256 - 16 * c], False, False))
-            ms.append(mm(d[:, 16 * c:16 * c + 16], T.BDr[:, :], T.E[:, 256 * c:256 * c + 16], False, c == 15))
-        op("P", ms, [("E",), ("BDr",), ("BD2",)], [("pb5",)])
+            ts(T.E[:, 256 * c:256 * c + n], T.fru[:, 16 * c:256], T.pb1[:, c:c + 1], A.is_equal, [("fru",), ("pb1",), ("w16",)],
+               [("E", 256 * c, 256 * c + n)], T.w16[:, c:c + 1], A.mult)
+            ms.append(mm(T.pb5[:, 16 * c:256], T.BD[:, :], T.E[:, 256 * c:256 * c + n], c == 0, c == 15))
+        op("P", ms, [("E", 256 * c0, 256 * c1), ("BD",)], [("pb5",)])
 
     def rwrites1(t):
         a = 1024 * t
-        op("P", [mm(T.pb7[:, 0:256], T.idH[:, :], T.Rd[:, 0:256], True, False), mm(T.pb7[:, 0:256], T.idH[:, :], T.VV[:, a:a + 256], False, True)],
-           [("Rd",), ("VV", a, a + 256), ("idH",)], [("pb7",)])
+        op("P", [mm(T.pb7[:, 0:256], T.idH[:, :], T.Rg[:, :], True, False), mm(T.pb7[:, 0:256], T.idH[:, :], T.VV[:, a:a + 256], False, True)],
+           [("Rg",), ("VV", a, a + 256), ("idH",)], [("pb7",)])
         n = 2048 + 512 * t
-        tt(T.Rt[:, n:n + 512:2], T.Rd[:, 0:256], T.winB[:, :], A.mult, [("Rd",), ("winB",)], [("Rt", n, n + 512, "even")])
+        tt(T.Rt[:, n:n + 512:2], T.Rg[:, :], T.winB[:, :], A.mult, [("Rg",), ("winB",)], [("Rt", n, n + 512, "even")])
 
     def rwrites2(t):
         n = 2048 + 512 * t
@@ -428,23 +442,26 @@ def rank_program(g, core, T, topo):
         tt(T.hF[:, :], T.hN[:, :], T.hM[:, :], A.add, [("hN",), ("hM",)], [("hF",)])
         cp(T.hp[:, :], T.hF[:, :], [("hF",)], [("hp",)])
 
-    def yp0b():
-        gather("S", T.Pg[:, :], ("Pg",), T.Ct[:, :], ("Ct",), T.hp[:, :], ("hp",))
-        block("pb2", 0, 64, T.QP, T.Pg, [("Pg",), ("QP",)])
+    def yp0b(h):
+        gather("S", T.Pg[:, 512 * h:512 * h + 512], ("Pg", 512 * h, 512 * h + 512), T.Ct[:, :], ("Ct",), T.hp[:, 32 * h:32 * h + 32], ("hp",))
+        if h == 1:
+            block("pb2", 192, 64, T.QP, T.Pg, [("Pg",), ("QP",)])
 
     def yp0c():
-        cp(T.ypF[:, 0:64], T.pb2[:, 0:64], [("pb2",)], [("ypF", 0, 64)])
+        cp(T.ypF[:, 0:64], T.pb2[:, 192:256], [("pb2",)], [("ypF", 0, 64)])
         dma("D", T.yp[:, 0:1024], T.ypF[:, 0:64], [("ypF", 0, 64)], [])
 
     for t in range(3):
         XT = XP[t]
         if t == 0:
             xg("S", 0, 0, 0, 512)
+            pgat(0, 1024)
+            psum(1024)
             xg("V", 0, 0, 512, 1024)
         for k in range(5):
             kid(0, k)
             cmpz(t, 0, k)
-            pediff(0)
+            pekids(0)
             op("P", mm(T.pb3[:, 0:256], T.BDf1[:, :], T.Kg[:, 0:256], k == 0, k == 4), [("Kg", 0, 256), ("BDf1",)], [("pb3",)])
             if t > 0 and k == 0:
                 hsum(t, 0)
@@ -452,48 +469,46 @@ def rank_program(g, core, T, topo):
             if t == 0 and k > 0:
                 plist(k + 1, 1024 if k < 4 else 256)
             kid(1, k)
-            if t == 0 and k == 0:
-                pgat(0, 1024)
-                late1()
             cmpz(t, 1, k)
             if t > 0 and k == 0:
                 hsum(t, 1)
             pecnt(1)
-            pediff(1)
-            direct("pb1", 0, 64, T.QP, T.Kg, 0, [("Kg",), ("QP",)], stop=False)
+            pekids(1)
             if k == 0:
                 if t == 0:
+                    late1()
                     plist(1, 1024)
                 else:
                     hlist()
             if t == 0 and k < 4:
-                if k < 3:
-                    pgat(k + 1, 1024)
-                else:
-                    pgat(4, 256)
-                xg("V", 0, k + 1, 256, 1024)
-                xg("S", 0, k + 1, 0, 256)
+                pgat(k + 1, 1024 if k < 3 else 256)
+                if NS0[k] < 1024:
+                    xg("V", 0, k + 1, NS0[k], 1024)
+                xg("S", 0, k + 1, 0, NS0[k])
+                if k == 0:
+                    late1b()
                 if k == 1:
-                    late2()
-                if k == 2:
                     late3()
                 if k == 3:
-                    late4()
+                    ts(T.Et[:, :], T.Et[:, :], -256.0, A.add, [("Et",)], [("Et",)])
             elif k < 4:
-                xg("V", t, k + 1, 768, 1024)
-                xg("S", t, k + 1, 0, 768)
-                if t == 1 and k == 2:
-                    yp0b()
+                xg("V", t, k + 1, NS1, 1024)
+                xg("S", t, k + 1, 0, NS1)
             elif t < 2:
                 xg("S", t, 5, 0, 256)
-            if t == 1 and k == 4:
-                yp0c()
+            if t == 2 and k == 4:
+                yp0b(0)
+            if t == 0 and k == 4:
+                late2()
             ts(T.bs[0:64, :], T.pb6[0:64, 0:128], 8.5, A.is_ge, [("pb6",)], [("bs",)])
-            tt(T.ts[0:64, :], T.pb0[0:64, 0:128], T.bs[0:64, :], A.mult, [("pb0",), ("bs",)], [("ts",)])
-            op("P", mm(T.pb1[:, 0:64], T.ts[0:64, :], T.idF[0:64, 0:64], False, True), [("ts",), ("idF",)], [("pb1",)])
+            tt(T.ts[0:64, :], T.pb0[0:64, 128:256], T.bs[0:64, :], A.mult, [("pb0",), ("bs",)], [("ts",)])
+            tt(T.F[0:64, :], T.pb0[0:64, 0:128], T.ts[0:64, :], A.add, [("pb0",), ("ts",)], [("F",)])
+            op("P", lambda: g.tensor.transpose(T.pb1[:, 0:64], T.F[0:64, :], T.idF[0:64, 0:64]), [("F",), ("idF",)], [("pb1",)])
+            if t == 0 and k < 4:
+                psum(1024 if k < 3 else 256)
             if t > 0:
-                if k == 0:
-                    hcopy()
+                if t == 1 and k == 4:
+                    late4()
                 if k == 1:
                     rwrites1(t - 1)
                 if k == 2:
@@ -505,66 +520,80 @@ def rank_program(g, core, T, topo):
             elif k == 4:
                 hsum(0, 0)
                 hsum(0, 1)
-                hcopy()
+                hlow()
+                hhigh()
             cp(T.fl[:, :], T.pb1[:, 0:64], [("pb1",)], [("fl",)])
-        l0, l1 = ("fl", 0, 32), ("fl", 32, 64)
+        l0, l1 = ("fl", 0, 16), ("fl", 16, 64)
+        gather("S", T.Rg[:, :], ("Rg",), T.Rt[:, :], ("Rt",), T.fl[:, 0:16], l0)
+        tt(T.bt[:, 256:1024], T.Rt[:, :].indirect(T.fl[:, 16:64]), T[XT][:, 256:1024], A.is_gt, [("Rt",), l1, (XT, 256, 1024)], [("bt", 256, 1024)])
         gather("S", T.K5[:, :], ("K5",), T.Kt[:, :], ("Kt",), T.fl[:, 0:16], l0)
-        tt(T.bt[:, 512:1024], T.Rt[:, :].indirect(T.fl[:, 32:64]), T[XT][:, 512:1024], A.is_gt, [("Rt",), l1, (XT, 512, 1024)], [("bt", 512, 1024)])
-        gather("S", T.Rd[:, :], ("Rd",), T.Rt[:, :], ("Rt",), T.fl[:, 0:32], l0)
+        op("P", [mm(T.pb7[:, 0:256], T.idB[:, :], T.Rg[:, :], True, False), mm(T.pb7[:, 0:256], T.idN[:, :], T[XT][:, 0:256], False, True)],
+           [("Rg",), (XT, 0, 256), ("idB",), ("idN",)], [("pb7",)])
         op("P", [mm(T.pb4[:, 0:256], T.BDs[:, :], T.K5[:, :], True, True), mm(T.pb4[:, 256:512], T.BDf2[:, :], T.K5[:, :], True, True)],
            [("K5",), ("BDs",), ("BDf2",)], [("pb4",)])
-        direct("pb6", 32, 32, T.Q97, T.bt, 512, [("bt", 512, 1024), ("Q97",)])
-        cp(T.fru[:, :], T.pb4[:, 0:256], [("pb4",)], [("fru",)])
-        op("P", [mm(T.pb7[:, :], T.idB[:, :], T.Rd[:, :], True, False), mm(T.pb7[:, :], T.idN[:, :], T[XT][:, 0:512], False, True)],
-           [("Rd",), (XT, 0, 512), ("idB",), ("idN",)], [("pb7",)])
+        act(T.bt[:, 0:256], T.pb7[:, 0:256], [("pb7",)], [("bt", 0, 256)], func=AF.Sign, bias=-0.5)
+        direct("pb6", 16, 48, T.Q97, T.bt, 256, [("bt", 256, 1024), ("Q97",)])
+        direct("pb6", 0, 16, T.Q48, T.bt, 0, [("bt", 0, 256), ("Q48",)])
         if t < 2:
             act(T.depB[:, :], T.pb3[:, 0:256], [("pb3",)], [("depB",)])
-        act(T.bt[:, 0:512], T.pb7[:, :], [("pb7",), C["neg"][1]] if "neg" in C else [("pb7",)], [("bt", 0, 512)], func=AF.Sign, bias=-0.5)
-        direct("pb6", 0, 32, T.Q48, T.bt, 0, [("bt", 0, 512), ("Q48",)])
-        eqs()
+        cp(T.fru[:, :], T.pb4[:, 0:256], [("pb4",)], [("fru",)])
+        eqs(0, NE)
         if t < 2:
             direct("pb2", 0, 16, T.Q1k, T.depB, 0, [("depB",), ("Q1k",)])
+        ms = [mm(T.pb4[:, 0:256], T.DM[:, 0:128], T.NDa[:, :], True, False), mm(T.pb4[:, 0:256], T.DM[:, 128:256], T.NDc[:, :], False, False),
+              mm(T.pb4[:, 0:256], T.DM[:, 256:384], T.NDt[:, 256 * t:256 * t + 256], False, False),
+              mm(T.pb4[:, 0:256], T.DM[:, 384:512], T.NDe[:, :], False, False), mm(T.pb4[:, 0:256], T.idMn[:, :], T.K5[:, :], False, True)]
+        op("P", ms, [("DM",), ("idMn",), ("NDa",), ("NDc",), ("NDe",), ("NDt",), ("K5",)], [("pb4",)])
         tt(T.ix0[:, :], T.pb6[:, 0:64], T.hsS[:, :], A.add, [("pb6",), ("hsS",)], [("ix0",)])
         ts(T.iy0[:, :], T.ix0[:, :], 2047, A.bitwise_and, [("ix0",)], [("iy0",)])
         cp(T.el[:, :], T.iy0[:, :], [("iy0",)], [("el",)])
-        outcome(t, 0)
-        op("P", [mm(T.pb3[:, 0:256], T.idM[:, :], T.NDt[:, 256 * t:256 * t + 256], True, False), mm(T.pb3[:, 0:256], T.idMn[:, :], T.K5[:, :], False, True)],
-           [("idM",), ("idMn",), ("NDt",), ("K5",)], [("pb3",)])
+        out1a(t)
+        out0(t)
+        eqs(NE, 10)
+        eqs(10, 16)
+        out1b()
+        out0c(t)
         v0 = ("VV", 1024 * t, 1024 * t + 256)
-        op("P", [mm(T.pb0[:, 0:256], T.idB[:, :], T.Rd[:, 0:256], True, False), mm(T.pb0[:, 0:256], T.idN[:, :], T.VV[:, 1024 * t:1024 * t + 256], False, True)],
-           [("Rd",), v0, ("idB",), ("idN",)], [("pb0",)])
-        act(T.aB[:, :], T.pb0[:, 0:256], [("pb0",)], [("aB",)], func=AF.Abs)
-        outcome(t, 1)
-        tt(T.qB[:, :], T.pb5[:, 0:256], T.thrR[:, :], A.is_ge, [("pb5",), ("thrR",)], [("qB",)])
-        tt(T.flB[:, :], T.pb4[:, 256:512], T.qB[:, :], A.is_equal, [("pb4",), ("qB",)], [("flB",)])
-        op("P", mm(T.pb5[:, 256:512], T.BD[:, :], T.aB[:, :], True, True), [("aB",), ("BD",)], [("pb5",)])
-        direct("pb6", 64, 16, T.QS, T.flB, 0, [("flB",), ("QS",)])
-        ts(T.thx[:, :], T.flB[:, :], C["thm"][0], A.mult, [("flB",), C["thm"][1]], [("thx",)], 1048576.0, A.add)
+        op("P", [mm(T.pb7[:, 0:256], T.idB[:, :], T.Rg[:, :], True, False), mm(T.pb7[:, 0:256], T.idN[:, :], T.VV[:, 1024 * t:1024 * t + 256], False, True)],
+           [("Rg",), v0, ("idB",), ("idN",)], [("pb7",)])
+        act(T.aB[:, :], T.pb7[:, 0:256], [("pb7",)], [("aB",)], func=AF.Abs)
+        sums1(t, "pb0", False)
+        out1c(t)
         if t < 2:
             tt(T.dO[:, :], T.pb2[:, 0:16], T.laneL[:, :], A.add, [("pb2",), ("laneL",)], [("dO",)])
+        tt(T.fd[:, :], T.pb1[:, 0:16], T.dumpL[:, :], A.subtract, [("pb1",), ("dumpL",)], [("fd",)])
+        if t < 2:
             cp(T.depU[:, :], T.dO[:, :], [("dO",)], [("depU",)])
             gather("S", T.xf[:, :], ("xf",), T[XT][:, 0:NXP], (XT, 0, NXP), T.depU[:, :], ("depU",))
-        tt(T.fd[:, :], T.pb1[:, 0:16], T.dumpL[:, :], A.subtract, [("pb1",), ("dumpL",)], [("fd",)])
+        tt(T.qB[:, :], T.pb5[:, 0:256], T.thrR[:, :], A.is_ge, [("pb5",), ("thrR",)], [("qB",)])
+        op("P", mm(T.pb5[:, 256:512], T.BD[:, :], T.aB[:, :], True, True), [("aB",), ("BD",)], [("pb5",)])
+        tt(T.flB[:, :], T.pb4[:, 256:512], T.qB[:, :], A.is_equal, [("pb4",), ("qB",)], [("flB",)])
+        direct("pb6", 64, 16, T.QS, T.flB, 0, [("flB",), ("QS",)])
+        ts(T.thx[:, :], T.flB[:, :], C["thm"][0], A.mult, [("flB",), C["thm"][1]], [("thx",)], 1048576.0, A.add)
         tt(T.winB[:, :], T.pb5[:, 256:512], T.thx[:, :], A.is_ge, [("pb5",), ("thx",)], [("winB",)])
         tt(T.fo[:, :], T.pb6[:, 64:80], T.fd[:, :], A.mult, [("pb6",), ("fd",)], [("fo",)])
+        tt(T.tK[:, :], T.pb4[:, 0:256], T.winB[:, :], A.mult, [("pb4",), ("winB",)], [("tK",)])
         tt(T.fp[:, :], T.fo[:, :], T.dumpL[:, :], A.add, [("fo",), ("dumpL",)], [("fp",)])
-        tt(T.tK[:, :], T.pb3[:, 0:256], T.winB[:, :], A.mult, [("pb3",), ("winB",)], [("tK",)])
         cp(T.offU[:, :], T.fp[:, :], [("fp",)], [("offU",)])
         tt(T.Kt[:, :].indirect(T.offU[:, :]), T.K5[:, :], T.tK[:, :], A.add, [("K5",), ("tK",), ("offU",)], [("Kt",)])
         if t < 2:
             cp(T.Zt[:, :].indirect(T.offU[:, :]), T.xf[:, :], [("xf",), ("offU",)], [("Zt",)])
         arrived(t, 0)
         arrived(t, 1)
-    block("pb3", 0, 224, T.QP, T.Kt, [("Kt",), ("QP",)])
-    act(T.ykA[:, :], T.pb3[:, 0:224], [("pb3",)], [("ykA",)])
-    dma("D", T.yk0[:, :], T.ykA[:, :], [("ykA",)], [])
     rwrites1(2)
     rwrites2(2)
     dma("D", T.yr[:, :], T.Rt[:, 2048:3584], [("Rt", 2048, 3584)], [])
-    block("pb4", 0, 224, T.QK1, T.Kt, [("Kt",), ("QK1",)])
-    act(T.ykB[:, :], T.pb4[:, 0:224], [("pb4",)], [("ykB",)])
-    dma("D", T.yk1[:, :], T.ykB[:, :], [("ykB",)], [])
     ypn(2, "XF")
+    block("pb3", 0, 224, T.QKK, T.Kt, [("Kt",), ("QKK",)])
+    cp(T.yA[:, :], T.pb3[:, 0:224], [("pb3",)], [("yA",)])
+    ts(T.yB[:, :], T.yA[:, :], 4095, A.bitwise_and, [("yA",)], [("yB",)])
+    ts(T.yC[:, :], T.yA[:, :], 12, A.arith_shift_right, [("yA",)], [("yC",)])
+    cp(T.ykA[:, :], T.yB[:, :], [("yB",)], [("ykA",)])
+    cp(T.ykB[:, :], T.yC[:, :], [("yC",)], [("ykB",)])
+    dma("D", T.yk0[:, :], T.ykA[:, :], [("ykA",)], [])
+    dma("D", T.yk1[:, :], T.ykB[:, :], [("ykB",)], [])
+    yp0b(1)
+    yp0c()
     for s in total:
         if seen.get(("G", s), 0) < total[s]:
             g.wait_ge(T.sem[s], total[s])

import math
from concourse.mybir import dt, AluOpType, AxisListType, ActivationFunctionType

A = AluOpType
AF = ActivationFunctionType
NE = 4
NS0 = (64, 320, 320, 1024)
NS1 = 800
NXP = 5 * 1024 + 256
SCRATCH = {}


def _sb(dtype, text):
    for w in text.split():
        n, c = w.split(":")
        SCRATCH[n] = ("sbuf", [128, int(c)], dtype)


_sb("bfloat16", "xs:4096 Pt:4096 Kt:4096 Zt:4096 Rt:3584 Et:2048 Ct:1024 XA:5376 XB:5376 XC:5376 XF:1024 VV:3072 Pg:1024 Kg:1024 "
    "bt:1024 tm:1024 mm:1024 K5:256 Rg:256 aB:256 E:4096 qB:256 flB:256 winB:256 tK:256 xf:256 depB:256 NDa:256 NDc:256 "
    "NDe:256 NDt:768 ones:144 zer:144 Q01:144 QP:144 QW:144 Q97:144 Q48:144 QS:144 Q1k:144 QKK:144 BD:128 BDs:128 BDf2:128 "
    "BDf1:128 idB:128 idN:128 idH:128 idS:128 idMn:128 DM:512 WK:16 dg:640 pg:512 cg:128 sfl:256 sfh:256 sfi:256")
_sb("float32", "onesF:128 idF:128 BDF:128 bs:128 ts:128 F:128 w16:16 hsS:64 thrR:256 thx:256 laneL:16 dumpL:16 fd:16 fo:16 fp:16 "
    "dO:16 col:16 thF:1 ypF:192 ykA:224 ykB:224 hF:64")
_sb("int32", "prevI:256 k0I:128 k1I:128 curI:64 startI:64 wI:1 thI:1 pI:1 pmI:1 pnI:1 ownI:128 own2:128 ti:1024 tc:128 ix0:64 "
    "iy0:64 yA:224 yB:224 yC:224 hI:64 hJ:64 hK:64 hM:64 hN:64 yI:64 yJ:64 avI:256")
_sb("uint16", "f0:64 fl:64 sl:384 hl:64 hp:64 el:64 fru:256 offU:16 depU:16")
for _i in range(8):
    SCRATCH["pb%d" % _i] = ("psum", [128, 512], "float32")

NDMA = 40
SEMAPHORES = ["sV", "sS", "sP", "sG", "loc"] + ["d%d" % i for i in range(NDMA)] + ["a%d%d" % (t, c) for t in range(3) for c in range(2)]


def rank_program(g, core, T, topo):
    rank = T.rank_of(core)
    if rank is None:
        return
    dst = T.cores[(rank + 1) % len(T.cores)]
    src = T.cores[(rank - 1) % len(T.cores)]

    def pairs(a, b):
        return topo.engines(a, b)[::2]

    QUEUE = {"V": g.vector, "S": g.scalar, "P": g.tensor, "G": g, "D": g.sync}
    SEM = {"V": "sV", "S": "sS", "P": "sP", "G": "sG"}
    total = {}
    seen = {}
    recs = {}
    ndma = [0]

    def norm(r):
        b = r[0]
        if b.startswith("pb"):
            return (b, 0, 512, None)
        if len(r) == 1:
            return (b, 0, SCRATCH[b][1][1], None)
        if len(r) == 3:
            return (b, r[1], r[2], None)
        return r

    def deps(q, isdma, reads, writes):
        need = {}
        for rs, w in ((reads, False), (writes, True)):
            for r in rs:
                b, lo, hi, tag = norm(r)
                ps = b.startswith("pb")
                for rec in recs.get(b, []):
                    if rec[2] <= lo or rec[1] >= hi:
                        continue
                    if tag is not None and rec[3] is not None and tag != rec[3]:
                        continue
                    if not ps and not w and not rec[0]:
                        continue
                    if rec[6] == q and not isdma:
                        if ps or w:
                            continue
                    need[rec[4]] = max(need.get(rec[4], 0), rec[5])
        for s in need:
            if seen.get((q, s), 0) < need[s]:
                QUEUE[q].wait_ge(T.sem[s], need[s])
                seen[(q, s)] = need[s]

    def note(q, reads, writes, sem, val):
        for r in reads:
            b, lo, hi, tag = norm(r)
            w = b.startswith("pb")
            if w:
                recs[b] = []
            lst = recs.setdefault(b, [])
            recs[b] = [x for x in lst if not ((not x[0]) and x[4] == sem and x[1] >= lo and x[2] <= hi and x[3] == tag)]
            recs[b].append([w, lo, hi, tag, sem, val, q])
        for r in writes:
            b, lo, hi, tag = norm(r)
            lst = recs.setdefault(b, [])
            recs[b] = [x for x in lst if not (x[1] >= lo and x[2] <= hi and (tag is None or x[3] == tag))]
            recs[b].append([True, lo, hi, tag, sem, val, q])

    def op(q, calls, reads, writes):
        deps(q, False, reads, writes)
        s = SEM[q]
        if not isinstance(calls, list):
            calls = [calls]
        for c in calls:
            c().then_inc(T.sem[s], 1)
            total[s] = total.get(s, 0) + 1
        note(q, reads, writes, s, total[s])

    def dma(q, out, in_, reads, writes):
        deps(q, True, reads, writes)
        s = "d%d" % ndma[0]
        ndma[0] += 1
        QUEUE[q].dma_start(out, in_).then_inc(T.sem[s], 16)
        total[s] = 16
        note(q + "dma", reads, writes, s, 16)

    V = g.vector

    def cp(out, in_, rd, wr):
        op("V", lambda: V.tensor_copy(out=out, in_=in_), rd, wr)

    def tt(out, a, b, o, rd, wr):
        op("V", lambda: V.tensor_tensor(out=out, in0=a, in1=b, op=o), rd, wr)

    def ts(out, a, s1, o1, rd, wr, s2=None, o2=None):
        if o2 is None:
            op("V", lambda: V.tensor_scalar(out=out, in0=a, scalar1=s1, scalar2=None, op0=o1), rd, wr)
        else:
            op("V", lambda: V.tensor_scalar(out=out, in0=a, scalar1=s1, scalar2=s2, op0=o1, op1=o2), rd, wr)

    def fill(name, lo, hi, v):
        op("V", lambda: V.memset(T[name][:, lo:hi], v), [], [(name, lo, hi)])

    def act(out, in_, rd, wr, func=AF.Copy, **kw):
        op("S", lambda: g.scalar.activation(out=out, in_=in_, func=func, **kw), rd, wr)

    def gather(eng, out, outr, win, winr, lst, lstr):
        if eng == "S":
            act(out, win.indirect(lst), [winr, lstr], [outr])
        else:
            cp(out, win.indirect(lst), [winr, lstr], [outr])

    def mm(out, l, r, st, sp):
        return lambda: g.tensor.matmul(out, l, r, st, sp)

    def direct(bank, col, n, Q, data, base, rd):
        b = T[bank]
        op("P", [mm(b[:, col:col + n], Q[:, 15 - r:143 - r], data[:, base + r:base + 16 * n:16], r == 0, r == 15)
                 for r in range(16)], rd, [(bank,)])

    def block(bank, col, n, Q, data, rd):
        b = T[bank]
        op("P", [mm(b[:, col:col + n], Q[:, 15 - r:143 - r], data[:, n * r:n * r + n], r == 0, r == 15) for r in range(16)],
           rd, [(bank,)])

    def iota(name, lo, hi, pattern, base, cm, small):
        ap = T[name][:, lo:hi]
        if small:
            op("G", lambda: g.iota(ap, pattern, base, cm, allow_small_or_imprecise_dtypes=True), [], [(name, lo, hi)])
        else:
            op("G", lambda: g.iota(ap, pattern, base, cm), [], [(name, lo, hi)])

    def sel(name, src, pattern, cmp, base, cm, n):
        op("G", lambda: g.affine_select(T[name][:, 0:n], T[src][:, 0:n], pattern, cmp, 0.0, base, cm), [(src, 0, n)], [(name, 0, n)])

    def put(name, n, pattern, entries, lo=0):
        for j, (base, v) in enumerate(entries):
            ap, r = (T.zer[:, 0:n], ("zer",)) if j == 0 else (T[name][:, lo:lo + n], (name, lo, lo + n))
            op("G", lambda ap=ap, base=base, v=v: g.affine_select(T[name][:, lo:lo + n], ap, pattern, A.not_equal, float(v), base, 1),
               [r], [(name, lo, lo + n)])

    def putQ(name, entries):
        put(name, 144, [[-16, 9], [1000, 16]], [(-15000 - i, v) for i, v in entries])

    def putB(name, entries):
        put(name, 128, [[-16, 8], [0, 16]], [(-i, v) for i, v in entries])

    def putD(name, lo, places, v=1.0):
        put(name, 128, [[-16, 8], [999, 16]], [(-1000 * i, v) for i in places], lo)

    C = {}

    def column(nm):
        i = len(C)
        C[nm] = (T.col[:, i:i + 1], ("col", i, i + 1))
        return C[nm]

    dma("D", T.prevI[:, :], T.prev[:, :], [], [("prevI",)])
    dma("D", T.k0I[:, :], T.kid0[:, :], [], [("k0I",)])
    dma("S", T.curI[:, :], T.cur[:, :], [], [("curI",)])
    dma("S", T.startI[:, :], T.start[:, :], [], [("startI",)])
    dma("D", T.k1I[:, :], T.kid1[:, :], [], [("k1I",)])
    dma("S", T.wI[:, :], T.w[:, :], [], [("wI",)])
    dma("D", T.xs[:, :], T.x[:, :], [], [("xs",)])
    dma("S", T.Zt[:, 0:2048], T.z[:, :], [], [("Zt", 0, 2048)])

    iota("pI", 0, 1, [[0, 1]], 0, 1, False)
    iota("sfl", 0, 256, [[1, 256]], 0, 0, True)
    iota("ownI", 0, 128, [[1, 128]], 0, 128, False)
    pm, pmr = column("pm")
    pe, per = column("pe")
    fill("ones", 0, 144, 1.0)
    fill("onesF", 0, 128, 1.0)
    ts(T.pmI[:, :], T.pI[:, :], 15, A.bitwise_and, [("pI",)], [("pmI",)])
    ts(T.pnI[:, :], T.pI[:, :], 7, A.bitwise_and, [("pI",)], [("pnI",)])
    fill("thI", 0, 1, 0)
    cp(pm, T.pmI[:, :], [("pmI",)], [pmr])
    ts(pe, T.pnI[:, :], 8.0, A.add, [("pnI",)], [per])
    fill("Zt", 2048, 4096, 0.0)
    fill("Kt", 0, 4096, 0.0)
    fill("zer", 0, 144, 0.0)
    ZU = ("Zt", 2048, 4096)
    act(T.sfh[:, :], T.sfl[:, :], [("sfl",), pmr], [("sfh",)], func=AF.Identity, scale=0.0, bias=pm)
    act(T.sfi[:, :], T.sfl[:, :], [("sfl",), per], [("sfi",)], func=AF.Identity, scale=0.0, bias=pe)
    act(T.Pt[:, 0:2048], T.Zt[:, 2048:4096], [ZU], [("Pt", 0, 2048)])
    act(T.Pt[:, 2048:4096], T.Zt[:, 2048:4096], [ZU], [("Pt", 2048, 4096)])

    sel("Q01", "ones", [[0, 9], [1, 16]], A.is_equal, -15, 0, 144)
    sel("Q01", "Q01", [[-16, 9], [0, 16]], A.is_ge, 0, 1, 144)
    sel("Q01", "Q01", [[16, 9], [0, 16]], A.is_ge, 15, -1, 144)
    putQ("QP", [(0, 1), (1, 256)])
    put("WK", 8, [[-16, 8]], [(0, 1), (-1, 256)], 0)
    put("WK", 8, [[-16, 8]], [(0, -1), (-1, -256), (-2, 1), (-3, 256)], 8)
    putB("BDf1", [(6, 1)])
    sel("idF", "onesF", [[-1, 128]], A.is_equal, 0, 1, 128)
    sel("BD", "ones", [[-16, 8], [0, 16]], A.is_ge, 0, 1, 128)
    sel("BD", "BD", [[16, 8], [0, 16]], A.is_ge, 15, -1, 128)
    iota("laneL", 0, 16, [[16, 16]], 0, 0, True)
    for nm, v in (("idB", 1.0), ("idN", -1.0), ("idH", 0.5), ("idS", -128.0)):
        put(nm, 128, [[-1, 128]], [(0, v)])
    putB("BDs", [(4, 1), (5, 256)])
    putB("BDf2", [(6, 2)])
    putQ("Q1k", [(0, 1024)])
    putQ("QS", [(0, 1)])
    iota("NDa", 0, 256, [[0, 2], [2, 128]], 0, 0, True)
    iota("NDc", 0, 256, [[0, 2], [2, 128]], 1, 0, True)
    iota("NDe", 0, 256, [[0, 256]], 1, 0, True)
    for t in range(3):
        iota("NDt", 256 * t, 256 * t + 256, [[1, 2], [0, 128]], 8 + 2 * t, 0, True)
    putD("DM", 0, (0,))
    putD("DM", 128, (2,))
    putD("DM", 256, (1, 3))
    putD("DM", 384, (6,))
    putD("idMn", 0, (0, 1, 2, 3, 6), -1.0)
    putQ("QKK", [(0, 1), (1, 256), (2, 4096), (3, 1048576)])

    def digits(name, n, tmp, to, out, oo):
        for j, (o, v) in enumerate(((A.bitwise_and, 255), (A.arith_shift_right, 8))):
            a, b = to + j * n, oo + j * n
            ts(T[tmp][:, a:a + n], T[name][:, :], v, o, [(name,)], [(tmp, a, a + n)])
            cp(T[out][:, b:b + n], T[tmp][:, a:a + n], [(tmp, a, a + n)], [(out, b, b + n)])

    cp(T.f0[:, :], T.startI[:, :], [("startI",)], [("f0",)])
    cp(T.sl[:, 0:64], T.curI[:, :], [("curI",)], [("sl", 0, 64)])
    digits("prevI", 256, "ti", 512, "pg", 0)
    dma("D", T.Pt[0:128:16, :], T.pg[:, 0:256], [("pg", 0, 256)], [("Pt", 0, 4096, "r0")])
    dma("D", T.Pt[1:128:16, :], T.pg[:, 256:512], [("pg", 256, 512)], [("Pt", 0, 4096, "r1")])
    ts(T.own2[:, :], T.ownI[:, :], 2047, A.bitwise_and, [("ownI",)], [("own2",)])
    digits("k0I", 128, "ti", 0, "dg", 0)
    digits("k1I", 128, "ti", 256, "dg", 256)
    tt(T.dg[:, 512:640], T.k0I[:, :], T.own2[:, :], A.not_equal, [("k0I",), ("own2",)], [("dg", 512, 640)])
    dma("D", T.Kt[4:128:16, :], T.sfl[:, :], [("sfl",)], [("Kt", 0, 4096, "r4")])
    dma("D", T.Kt[5:128:16, :], T.sfh[:, :], [("sfh",)], [("Kt", 0, 4096, "r5")])
    for i in range(4):
        nm = ("sfl", "sfi")[i % 2]
        dma("D", T.Kt[i:128:16, 2048:4096], T[nm][0:64, :], [(nm,)], [("Kt", 2048, 4096, "r%d" % i)])
    for i, j in ((0, 0), (1, 1), (2, 2), (3, 3), (6, 4)):
        dma("D", T.Kt[i:128:16, 0:2048], T.dg[:, 128 * j:128 * j + 128], [("dg", 128 * j, 128 * j + 128)], [("Kt", 0, 2048, "r%d" % i)])
    dma("D", T.thI[0:128:16, :], T.th[:, :], [], [("thI",)])
    dma("D", T.Rt[:, 0:2048], T.rs[:, :], [], [("Rt", 0, 2048)])
    dma("D", T.Et[:, :], T.env[:, :], [], [("Et",)])
    wc, wcr = column("w")
    cp(wc, T.wI[:, :], [("wI",)], [wcr])
    W1 = T.Q01[:, 15:128:16]

    def scaled(name, c, rd):
        ts(T[name][:, :], T.Q01[:, :], c, A.mult, [("Q01",)] + rd, [(name,)])

    LN = math.log(1.85)

    def late1():
        fill("Rt", 2048, 3584, 0.0)
        fill("Ct", 0, 1024, 0.0)
        scaled("QW", wc, [wcr])

    def late1b():
        ts(T.laneL[:, :], T.laneL[:, :], pm, A.add, [("laneL",), pmr], [("laneL",)])
        scaled("Q97", 97.0, [])
        scaled("Q48", 48.5, [])
        ts(T.dumpL[:, :], T.laneL[:, :], 3584.0, A.add, [("laneL",)], [("dumpL",)])

    def late2():
        act(T.w16[:, :], T.laneL[:, :], [("laneL",)], [("w16",)], func=AF.Exp, scale=-LN, bias=128 * LN)
        act(T.thrR[:, :], T.sfl[:, :], [("sfl",)], [("thrR",)], func=AF.Exp, scale=-LN, bias=128 * LN + math.log(2.5))

    def late3():
        cp(T.BDF[:, :], T.BD[:, :], [("BD",)], [("BDF",)])
        cp(T.thF[:, :], T.thI[:, :], [("thI",)], [("thF",)])
        op("P", mm(T.pb4[:, 100:101], T.BDF[:, :], T.thF[:, :], True, True), [("BDF",), ("thF",)], [("pb4",)])
        c, r = column("thm")
        ts(c, T.pb4[:, 100:101], -1048576.0, A.add, [("pb4",)], [r])

    def late4():
        digits("curI", 64, "tc", 0, "cg", 0)
        dma("D", T.Ct[0:128:16, :], T.cg[:, 0:64], [("cg", 0, 64)], [("Ct", 0, 1024, "r0")])
        dma("D", T.Ct[1:128:16, :], T.cg[:, 64:128], [("cg", 64, 128)], [("Ct", 0, 1024, "r1")])

    XP = ["XA", "XB", "XC", "XF"]

    def nodes(h, k):
        nm = "f0" if k == 0 else "fl"
        return T[nm][:, 32 * h:32 * h + 32], (nm, 32 * h, 32 * h + 32)

    def kid(h, k):
        l, r = nodes(h, k)
        act(T.Kg[:, 512 * h:512 * h + 512], T.Kt[:, :].indirect(l), [("Kt",), r], [("Kg", 512 * h, 512 * h + 512)])

    def cmpz(t, h, k):
        l, r = nodes(h, k)
        a = 1024 * k + 512 * h
        tt(T.bt[:, 512 * h:512 * h + 512], T.Zt[:, :].indirect(l), T[XP[t]][:, a:a + 512], A.is_le,
           [("Zt",), r, (XP[t], a, a + 512)], [("bt", 512 * h, 512 * h + 512)])

    def pekids(h):
        op("P", [mm(T.pb0[32 * h:32 * h + 32, r:256:16], T.Kg[:, 512 * h + r:512 * h + 512:16], T.WK[:, :], True, True) for r in range(16)],
           [("Kg", 512 * h, 512 * h + 512), ("WK",)], [("pb0",)])

    def pecnt(h):
        op("P", [mm(T.pb6[32 * h:32 * h + 32, r:128:16], T.bt[:, 512 * h + r:512 * h + 512:16], W1, True, True) for r in range(16)],
           [("bt", 512 * h, 512 * h + 512), ("Q01",)], [("pb6",)])

    def xg(eng, t, k, a, b):
        o = 1024 * k
        out, outr = T[XP[t]][:, o + a:o + b], (XP[t], o + a, o + b)
        if t == 0:
            lo, hi = 64 * k + a // 16, 64 * k + b // 16
            gather(eng, out, outr, T.xs[:, :], ("xs",), T.sl[:, lo:hi], ("sl", lo, hi))
        else:
            w = 1024 * (k - 1)
            gather(eng, out, outr, T[XP[t - 1]][:, w:w + 1024], (XP[t - 1], w, w + 1024), T.hl[:, a // 16:b // 16], ("hl", a // 16, b // 16))

    def pgat(k, n):
        gather("S", T.Pg[:, 0:n], ("Pg",), T.Pt[:, :], ("Pt",), T.sl[:, 64 * k:64 * k + n // 16], ("sl", 64 * k, 64 * k + n // 16))

    def psum(n):
        direct("pb2", 0, n // 16, T.QP, T.Pg, 0, [("Pg",), ("QP",)])

    def plist(k, n):
        cp(T.sl[:, 64 * k:64 * k + n // 16], T.pb2[:, 0:n // 16], [("pb2",)], [("sl", 64 * k, 64 * k + n // 16)])

    def hsum(t, h):
        direct("pb2", 64 + 32 * h, 32, T.QW, T[XP[t]], 512 * h, [(XP[t], 512 * h, 512 * h + 512), ("QW",)])

    def hlow():
        ts(T.hsS[:, 0:16], T.pb2[:, 64:80], 776.0, A.add, [("pb2",)], [("hsS", 0, 16)])

    def hhigh():
        cp(T.hsS[:, 16:64], T.pb2[:, 80:128], [("pb2",)], [("hsS", 16, 64)])

    def hlist():
        cp(T.hI[:, :], T.pb2[:, 64:128], [("pb2",)], [("hI",)])
        hlow()
        ts(T.hJ[:, :], T.hI[:, :], 1023, A.bitwise_and, [("hI",)], [("hJ",)])
        hhigh()
        cp(T.hl[:, :], T.hJ[:, :], [("hJ",)], [("hl",)])

    def arrived(t, h):
        s = "a%d%d" % (t, h)
        total[s] = len(pairs(src, core))
        recs.setdefault(XP[t + 1], []).append([True, 512 * h, 512 * h + 512, None, s, total[s], "remote"])

    def send(t, h):
        a, b = 1024 * t + 512 * h, 1024 * t + 512 * h + 512
        deps("G", True, [("VV", a, b)], [])
        en = pairs(core, dst)
        mask = sum(1 << x for x in en)
        rid, pid, _ = topo.addr(dst)
        g.remote_dma(out_ap=T[XP[t + 1]][:, 512 * h:512 * h + 512], in_ap=T.VV[:, a:b], remote_sem=T.sem["a%d%d" % (t, h)],
                     local_sem=T.sem.loc, pid=pid, routing_id=rid, dma_engine_mask=mask)
        total["loc"] = total.get("loc", 0) + len(en)

    def out0(t):
        tt(T.tm[:, 0:512], T.Et[:, :].indirect(T.el[:, 0:32]), T[XP[t]][:, 0:512], A.add,
           [("Et",), ("el",), (XP[t], 0, 512)], [("tm", 0, 512)])
        ts(T.mm[:, 0:512], T.tm[:, 0:512], 0.0, A.is_lt, [("tm", 0, 512)], [("mm", 0, 512)], 256.0, A.mult)
        op("P", [mm(T.pb7[:, :], T.idB[:, :], T.tm[:, 0:512], True, False), mm(T.pb7[:, :], T.idB[:, :], T.mm[:, 0:512], False, True)],
           [("tm", 0, 512), ("mm", 0, 512), ("idB",)], [("pb7",)])

    def out0c(t):
        act(T.VV[:, 1024 * t:1024 * t + 512], T.pb7[:, :], [("pb7",)], [("VV", 1024 * t, 1024 * t + 512)])
        send(t, 0)

    def sums1(t, bank, stop):
        op("P", [mm(T[bank][:, :], T.idB[:, :], T.tm[:, 512:1024], True, False),
                 mm(T[bank][:, :], T.idB[:, :], T[XP[t]][:, 512:1024], False, stop)],
           [("tm", 512, 1024), (XP[t], 512, 1024), ("idB",)], [(bank,)])

    def out1a(t):
        gather("S", T.tm[:, 512:1024], ("tm", 512, 1024), T.Et[:, :], ("Et",), T.el[:, 32:64], ("el",))
        sums1(t, "pb3", True)

    def out1b():
        act(T.mm[:, 512:1024], T.pb3[:, :], [("pb3",)], [("mm", 512, 1024)], func=AF.Sign, bias=0.5)

    def out1c(t):
        op("P", mm(T.pb0[:, :], T.idS[:, :], T.mm[:, 512:1024], False, True), [("mm", 512, 1024), ("idS",)], [("pb0",)])
        act(T.VV[:, 1024 * t + 512:1024 * t + 1024], T.pb0[:, :], [("pb0",)], [("VV", 1024 * t + 512, 1024 * t + 1024)], bias=128.0)
        send(t, 1)

    def eqs(c0, c1):
        ms = []
        for c in range(c0, c1):
            n = 256 - 16 * c
            ts(T.E[:, 256 * c:256 * c + n], T.fru[:, 16 * c:256], T.pb1[:, c:c + 1], A.is_equal, [("fru",), ("pb1",), ("w16",)],
               [("E", 256 * c, 256 * c + n)], T.w16[:, c:c + 1], A.mult)
            ms.append(mm(T.pb5[:, 16 * c:256], T.BD[:, :], T.E[:, 256 * c:256 * c + n], c == 0, c == 15))
        op("P", ms, [("E", 256 * c0, 256 * c1), ("BD",)], [("pb5",)])

    def rwrites1(t):
        a = 1024 * t
        op("P", [mm(T.pb7[:, 0:256], T.idH[:, :], T.Rg[:, :], True, False), mm(T.pb7[:, 0:256], T.idH[:, :], T.VV[:, a:a + 256], False, True)],
           [("Rg",), ("VV", a, a + 256), ("idH",)], [("pb7",)])
        n = 2048 + 512 * t
        tt(T.Rt[:, n:n + 512:2], T.Rg[:, :], T.winB[:, :], A.mult, [("Rg",), ("winB",)], [("Rt", n, n + 512, "even")])

    def rwrites2(t):
        n = 2048 + 512 * t
        ts(T.avI[:, :], T.pb7[:, 0:256], -0.25, A.add, [("pb7",)], [("avI",)])
        tt(T.Rt[:, n + 1:n + 512:2], T.avI[:, :], T.winB[:, :], A.mult, [("avI",), ("winB",)], [("Rt", n, n + 512, "odd")])

    def ypn(t, xn):
        block("pb2", 128, 64, T.QW, T[xn], [(xn, 0, 1024), ("QW",)])
        cp(T.yI[:, :], T.pb2[:, 128:192], [("pb2",)], [("yI",)])
        ts(T.yJ[:, :], T.yI[:, :], 1023, A.bitwise_and, [("yI",)], [("yJ",)])
        ts(T.ypF[:, 64 * t:64 * t + 64], T.yJ[:, :], float(4096 + 1024 * (t - 1)), A.add, [("yJ",)], [("ypF", 64 * t, 64 * t + 64)])
        dma("D", T.yp[:, 1024 * t:1024 * t + 1024], T.ypF[:, 64 * t:64 * t + 64], [("ypF", 64 * t, 64 * t + 64)], [])

    def yp0a():
        ts(T.hK[:, :], T.hJ[:, :], 15, A.bitwise_and, [("hJ",)], [("hK",)])
        ts(T.hM[:, :], T.hJ[:, :], 4, A.arith_shift_right, [("hJ",)], [("hM",)])
        ts(T.hN[:, :], T.hK[:, :], 64.0, A.mult, [("hK",)], [("hN",)])
        tt(T.hF[:, :], T.hN[:, :], T.hM[:, :], A.add, [("hN",), ("hM",)], [("hF",)])
        cp(T.hp[:, :], T.hF[:, :], [("hF",)], [("hp",)])

    def yp0b(h):
        gather("S", T.Pg[:, 512 * h:512 * h + 512], ("Pg", 512 * h, 512 * h + 512), T.Ct[:, :], ("Ct",), T.hp[:, 32 * h:32 * h + 32], ("hp",))
        if h == 1:
            block("pb2", 192, 64, T.QP, T.Pg, [("Pg",), ("QP",)])

    def yp0c():
        cp(T.ypF[:, 0:64], T.pb2[:, 192:256], [("pb2",)], [("ypF", 0, 64)])
        dma("D", T.yp[:, 0:1024], T.ypF[:, 0:64], [("ypF", 0, 64)], [])

    for t in range(3):
        XT = XP[t]
        if t == 0:
            xg("S", 0, 0, 0, 512)
            pgat(0, 1024)
            psum(1024)
            xg("V", 0, 0, 512, 1024)
        for k in range(5):
            kid(0, k)
            cmpz(t, 0, k)
            pekids(0)
            op("P", mm(T.pb3[:, 0:256], T.BDf1[:, :], T.Kg[:, 0:256], k == 0, k == 4), [("Kg", 0, 256), ("BDf1",)], [("pb3",)])
            if t > 0 and k == 0:
                hsum(t, 0)
            pecnt(0)
            if t == 0 and k > 0:
                plist(k + 1, 1024 if k < 4 else 256)
            kid(1, k)
            cmpz(t, 1, k)
            if t > 0 and k == 0:
                hsum(t, 1)
            pecnt(1)
            pekids(1)
            if k == 0:
                if t == 0:
                    late1()
                    plist(1, 1024)
                else:
                    hlist()
            if t == 0 and k < 4:
                pgat(k + 1, 1024 if k < 3 else 256)
                if NS0[k] < 1024:
                    xg("V", 0, k + 1, NS0[k], 1024)
                xg("S", 0, k + 1, 0, NS0[k])
                if k == 0:
                    late1b()
                if k == 1:
                    late3()
                if k == 3:
                    ts(T.Et[:, :], T.Et[:, :], -256.0, A.add, [("Et",)], [("Et",)])
            elif k < 4:
                xg("V", t, k + 1, NS1, 1024)
                xg("S", t, k + 1, 0, NS1)
            elif t < 2:
                xg("S", t, 5, 0, 256)
            if t == 2 and k == 4:
                yp0b(0)
            if t == 0 and k == 4:
                late2()
            ts(T.bs[0:64, :], T.pb6[0:64, 0:128], 8.5, A.is_ge, [("pb6",)], [("bs",)])
            tt(T.ts[0:64, :], T.pb0[0:64, 128:256], T.bs[0:64, :], A.mult, [("pb0",), ("bs",)], [("ts",)])
            tt(T.F[0:64, :], T.pb0[0:64, 0:128], T.ts[0:64, :], A.add, [("pb0",), ("ts",)], [("F",)])
            op("P", lambda: g.tensor.transpose(T.pb1[:, 0:64], T.F[0:64, :], T.idF[0:64, 0:64]), [("F",), ("idF",)], [("pb1",)])
            if t == 0 and k < 4:
                psum(1024 if k < 3 else 256)
            if t > 0:
                if t == 1 and k == 4:
                    late4()
                if k == 1:
                    rwrites1(t - 1)
                if k == 2:
                    rwrites2(t - 1)
                if t == 1 and k == 1:
                    yp0a()
                if t == 2 and k == 3:
                    ypn(1, "XC")
            elif k == 4:
                hsum(0, 0)
                hsum(0, 1)
                hlow()
                hhigh()
            cp(T.fl[:, :], T.pb1[:, 0:64], [("pb1",)], [("fl",)])
        l0, l1 = ("fl", 0, 16), ("fl", 16, 64)
        gather("S", T.Rg[:, :], ("Rg",), T.Rt[:, :], ("Rt",), T.fl[:, 0:16], l0)
        tt(T.bt[:, 256:1024], T.Rt[:, :].indirect(T.fl[:, 16:64]), T[XT][:, 256:1024], A.is_gt, [("Rt",), l1, (XT, 256, 1024)], [("bt", 256, 1024)])
        gather("S", T.K5[:, :], ("K5",), T.Kt[:, :], ("Kt",), T.fl[:, 0:16], l0)
        op("P", [mm(T.pb7[:, 0:256], T.idB[:, :], T.Rg[:, :], True, False), mm(T.pb7[:, 0:256], T.idN[:, :], T[XT][:, 0:256], False, True)],
           [("Rg",), (XT, 0, 256), ("idB",), ("idN",)], [("pb7",)])
        op("P", [mm(T.pb4[:, 0:256], T.BDs[:, :], T.K5[:, :], True, True), mm(T.pb4[:, 256:512], T.BDf2[:, :], T.K5[:, :], True, True)],
           [("K5",), ("BDs",), ("BDf2",)], [("pb4",)])
        act(T.bt[:, 0:256], T.pb7[:, 0:256], [("pb7",)], [("bt", 0, 256)], func=AF.Sign, bias=-0.5)
        direct("pb6", 16, 48, T.Q97, T.bt, 256, [("bt", 256, 1024), ("Q97",)])
        direct("pb6", 0, 16, T.Q48, T.bt, 0, [("bt", 0, 256), ("Q48",)])
        if t < 2:
            act(T.depB[:, :], T.pb3[:, 0:256], [("pb3",)], [("depB",)])
        cp(T.fru[:, :], T.pb4[:, 0:256], [("pb4",)], [("fru",)])
        eqs(0, NE)
        if t < 2:
            direct("pb2", 0, 16, T.Q1k, T.depB, 0, [("depB",), ("Q1k",)])
        ms = [mm(T.pb4[:, 0:256], T.DM[:, 0:128], T.NDa[:, :], True, False), mm(T.pb4[:, 0:256], T.DM[:, 128:256], T.NDc[:, :], False, False),
              mm(T.pb4[:, 0:256], T.DM[:, 256:384], T.NDt[:, 256 * t:256 * t + 256], False, False),
              mm(T.pb4[:, 0:256], T.DM[:, 384:512], T.NDe[:, :], False, False), mm(T.pb4[:, 0:256], T.idMn[:, :], T.K5[:, :], False, True)]
        op("P", ms, [("DM",), ("idMn",), ("NDa",), ("NDc",), ("NDe",), ("NDt",), ("K5",)], [("pb4",)])
        tt(T.ix0[:, :], T.pb6[:, 0:64], T.hsS[:, :], A.add, [("pb6",), ("hsS",)], [("ix0",)])
        ts(T.iy0[:, :], T.ix0[:, :], 2047, A.bitwise_and, [("ix0",)], [("iy0",)])
        cp(T.el[:, :], T.iy0[:, :], [("iy0",)], [("el",)])
        out1a(t)
        out0(t)
        eqs(NE, 10)
        eqs(10, 16)
        out1b()
        out0c(t)
        v0 = ("VV", 1024 * t, 1024 * t + 256)
        op("P", [mm(T.pb7[:, 0:256], T.idB[:, :], T.Rg[:, :], True, False), mm(T.pb7[:, 0:256], T.idN[:, :], T.VV[:, 1024 * t:1024 * t + 256], False, True)],
           [("Rg",), v0, ("idB",), ("idN",)], [("pb7",)])
        act(T.aB[:, :], T.pb7[:, 0:256], [("pb7",)], [("aB",)], func=AF.Abs)
        sums1(t, "pb0", False)
        out1c(t)
        if t < 2:
            tt(T.dO[:, :], T.pb2[:, 0:16], T.laneL[:, :], A.add, [("pb2",), ("laneL",)], [("dO",)])
        tt(T.fd[:, :], T.pb1[:, 0:16], T.dumpL[:, :], A.subtract, [("pb1",), ("dumpL",)], [("fd",)])
        if t < 2:
            cp(T.depU[:, :], T.dO[:, :], [("dO",)], [("depU",)])
            gather("S", T.xf[:, :], ("xf",), T[XT][:, 0:NXP], (XT, 0, NXP), T.depU[:, :], ("depU",))
        tt(T.qB[:, :], T.pb5[:, 0:256], T.thrR[:, :], A.is_ge, [("pb5",), ("thrR",)], [("qB",)])
        op("P", mm(T.pb5[:, 256:512], T.BD[:, :], T.aB[:, :], True, True), [("aB",), ("BD",)], [("pb5",)])
        tt(T.flB[:, :], T.pb4[:, 256:512], T.qB[:, :], A.is_equal, [("pb4",), ("qB",)], [("flB",)])
        direct("pb6", 64, 16, T.QS, T.flB, 0, [("flB",), ("QS",)])
        ts(T.thx[:, :], T.flB[:, :], C["thm"][0], A.mult, [("flB",), C["thm"][1]], [("thx",)], 1048576.0, A.add)
        tt(T.winB[:, :], T.pb5[:, 256:512], T.thx[:, :], A.is_ge, [("pb5",), ("thx",)], [("winB",)])
        tt(T.fo[:, :], T.pb6[:, 64:80], T.fd[:, :], A.mult, [("pb6",), ("fd",)], [("fo",)])
        tt(T.tK[:, :], T.pb4[:, 0:256], T.winB[:, :], A.mult, [("pb4",), ("winB",)], [("tK",)])
        tt(T.fp[:, :], T.fo[:, :], T.dumpL[:, :], A.add, [("fo",), ("dumpL",)], [("fp",)])
        cp(T.offU[:, :], T.fp[:, :], [("fp",)], [("offU",)])
        tt(T.Kt[:, :].indirect(T.offU[:, :]), T.K5[:, :], T.tK[:, :], A.add, [("K5",), ("tK",), ("offU",)], [("Kt",)])
        if t < 2:
            cp(T.Zt[:, :].indirect(T.offU[:, :]), T.xf[:, :], [("xf",), ("offU",)], [("Zt",)])
        arrived(t, 0)
        arrived(t, 1)
    rwrites1(2)
    rwrites2(2)
    dma("D", T.yr[:, :], T.Rt[:, 2048:3584], [("Rt", 2048, 3584)], [])
    ypn(2, "XF")
    block("pb3", 0, 224, T.QKK, T.Kt, [("Kt",), ("QKK",)])
    cp(T.yA[:, :], T.pb3[:, 0:224], [("pb3",)], [("yA",)])
    ts(T.yB[:, :], T.yA[:, :], 4095, A.bitwise_and, [("yA",)], [("yB",)])
    ts(T.yC[:, :], T.yA[:, :], 12, A.arith_shift_right, [("yA",)], [("yC",)])
    cp(T.ykA[:, :], T.yB[:, :], [("yB",)], [("ykA",)])
    cp(T.ykB[:, :], T.yC[:, :], [("yC",)], [("ykB",)])
    dma("D", T.yk0[:, :], T.ykA[:, :], [("ykA",)], [])
    dma("D", T.yk1[:, :], T.ykB[:, :], [("ykB",)], [])
    yp0b(1)
    yp0c()
    for s in total:
        if seen.get(("G", s), 0) < total[s]:
            g.wait_ge(T.sem[s], total[s])
